import numpy as np, ml_dtypes
CORES = [3,11,19,27,35,43,51,59]
N = 8
BF = ml_dtypes.bfloat16
W, S, RO, LIM = 4096, 192, 3, 5
HEARER = [[1, 0, 3, 2, 5, 4, 7, 6], [2, 3, 0, 1, 6, 7, 4, 5], [4, 5, 6, 7, 0, 1, 2, 3]]
def world(rng, skew):
    m = rng.integers(2, 5, (8, 1, 1)); pn = rng.integers(2, 9, (1, 8, 1)); noise = 0.05 + 0.45 * rng.random((N, 8, 1, 1))
    alph = np.argsort(rng.random((8, 16, 513)), axis=-1)[..., :4] - 256
    proto = (rng.random((8, 8, 16)) * m).astype(np.int64); z = (rng.random((N, 8, W)) * pn).astype(np.int64)
    e = proto[np.arange(8)[None, :, None], z]
    u = (rng.random(e.shape, dtype=np.float32) ** skew * m).astype(np.int64)
    e = np.where(rng.random(e.shape, dtype=np.float32) < noise, np.minimum(u, 3), e)
    return np.ascontiguousarray(alph[np.arange(8)[None, :, None, None], np.arange(16), e].transpose(0, 1, 3, 2))
def parts(rng, skew=1):
    X = world(rng, skew)
    As = np.minimum((W * rng.random((N, 8, 16, W)) ** skew).astype(np.int64), W - 1)
    C = np.minimum((W * rng.random((N, 8, 16, S)) ** skew).astype(np.int64), W - 1); H = np.minimum((W * rng.random((N, 8, 16, S)) ** skew).astype(np.int64), W - 1)
    R = np.argsort(rng.random((N, 8, 16, S)), axis=2); A = np.minimum((256 * rng.random((N, 8, S)) ** skew).astype(np.int64), 255)
    return X, As, C, H, R, A
def pack(X, As, C, H, R, A):
    return {"x": np.ascontiguousarray(X.reshape(N, 128, W)).astype(np.float32).astype(BF), "assoc": np.ascontiguousarray(As.reshape(N, 128, W)).astype(np.int32),
            "ctx": np.ascontiguousarray(C.reshape(N, 128, S)).astype(np.int32), "cand": np.ascontiguousarray(H.reshape(N, 128, S)).astype(np.int32),
            "pref": np.ascontiguousarray(R.reshape(N, 128, S)).astype(np.int32), "fail0": np.ascontiguousarray(A).astype(np.int32)}
def setup_inputs(rng):
    return pack(*parts(rng))
def setup_inputs_spread(rng):
    X, As, C, H, R, A = parts(rng, 3)
    X = np.where((X == X[0, :, :, :1]) & (rng.random((8, 16, 1)) < 0.5), 0, X)
    share = 0.05 + 0.4 * rng.random((N, 8, 1, 1))
    X = np.where(rng.random((N, 8, 1, W)) < share, rng.integers(-256, 257, X.shape), X)
    X = np.where((X == 0) & (rng.random(X.shape, dtype=np.float32) < 0.5), -0.0, X)
    return pack(X, As, C, H, R, A)
def endlist(rng, shape):
    return np.where(rng.random(shape) < 0.68, rng.choice(np.array([0, W - 1]), shape), rng.integers(0, W, shape))
def setup_inputs_ends(rng):
    proto = rng.choice(np.array([-1, 1]), (8, 6, 16)); e = proto[np.arange(8)[None, :, None], rng.integers(0, 6, (N, 8, W))]
    e = np.where(rng.random(e.shape, dtype=np.float32) < 0.05 + 0.3 * rng.random((N, 8, 1, 1)), -e, e)
    u = rng.random((N, 8, W, 1)); e = np.where(u < 0.15, 1, np.where(u < 0.3, -1, e))
    X = np.ascontiguousarray(256 * e.transpose(0, 1, 3, 2)); sg = 256 * rng.choice(np.array([-1, 1]), (8, 1)); a = np.arange(16)[:, None]
    X[..., 0] = -sg; X[..., W - 1] = sg
    X[..., W - 16:W - 1] = sg[:, :, None] * np.where(np.arange(16)[:, None] == np.arange(1, 16), -1, 1)
    X[..., 1:16] = -X[..., W - 16:W - 1]
    X[..., 16:32] = sg[:, :, None] * np.where((a >= 1) & (a <= np.arange(16)), 1, -1)
    As = endlist(rng, (N, 8, 16, W)); C = endlist(rng, (N, 8, 16, S)); H = endlist(rng, (N, 8, 16, S))
    C[..., S - 8:] = np.concatenate([np.array([W - 1]), np.arange(W - 16, W - 1)])[:, None]
    H[..., S - 3:] = 0; H[:, :, 15, S - 1] = W - 1; H[:, :, 14:, S - 3] = W - 1
    C[..., S - 4] = a[:, 0]; H[..., S - 4] = W - 1
    H[..., S - 8:S - 4] = 31 - np.arange(11, 15) - (a < rng.integers(1, 16, (N, 8, 1, 4)))
    C[..., 0] = W - 1; C[:, :, 0, 0] = 0; H[..., 0] = W - 1
    C[..., 1] = W - 1; H[..., 1] = 0
    R = np.where(rng.random((N, 8, 1, S)) < 0.5, a, 15 - a); R = np.where(rng.random((N, 8, 1, S)) < 0.25, np.argsort(rng.random((N, 8, 16, S)), axis=2), R)
    return pack(X, As, C, H, R, rng.choice(np.array([0, 255]), (N, 8, S)))
def setup_inputs_corners(rng):
    X, As, C, H, R, A = parts(rng); k = np.arange(16); kk = k[:, None]; o = np.arange(1, S, 2); M = len(o); sp = np.argsort(np.array(HEARER[0]))
    A = rng.choice(np.array([0, 1, 2, 3, 252, 253, 254, 255]), (N, 8, S))
    R = np.where(rng.random((N, 8, 1, S)) < 0.3, np.where(rng.random((N, 8, 1, S)) < 0.5, kk, 15 - kk), R)
    rk = R[..., o].transpose(0, 1, 3, 2)[:, :, :, None, :]
    kind = rng.integers(0, 4, (N, 8, M, 1, 1)); b = rng.integers(-256, 256, (N, 8, M, 1, 16))
    one = (rk == kk) | ((rk > kk) & (rng.random((N, 8, M, 16, 16)) < 0.5))
    dx = (((kind == 1) & one) | (kind == 2) | ((kind == 3) & (rk == 15) & (kk >= 8))) & (kk > 0)
    room = (LIM + (A[..., o] & 3))[..., None, None]; how = rng.integers(0, 4, (N, 8, M, 1, 1))
    m = np.where(how == 0, 0, np.where(how == 1, room, np.where(how == 2, room + 1, 16)))
    w = np.where(kind == 0, 0, rng.choice(np.array([0, 1, 14, 15]), (N, 8, M, 1, 1)))
    dy = np.where(kind == 3, rk < m, rk >= 16 - m) | (kk < w)
    cols = (16 * o[:, None] + k).reshape(-1)
    X[..., cols] = (b + dx).transpose(0, 1, 4, 2, 3).reshape(N, 8, 16, 16 * M)
    X[..., cols - 16] = (b + dy).transpose(0, 1, 4, 2, 3).reshape(N, 8, 16, 16 * M)[sp]
    C[..., o] = 16 * o + kk; H[..., o] = 16 * (o - 1) + kk
    C[:, 6, :, 0::2] = C[:, 6, :1, 0::2]; H[:, 2, :, 0::2] = H[:, 2, :1, 0::2]
    As[:, 3] = np.where(rng.random((N, 16, W)) < 0.5, np.arange(W), As[:, 3]); As[:, 5] = rng.choice(np.array([0, W - 1]), (N, 16, W))
    return pack(X, As, C, H, R, A)
def setup_inputs_bulk(rng):
    X, As, C, H, R, A = parts(rng); h = W // 2; v = h // 2; m = min(LIM, 8)
    ga, gb, gc, gd, ge = [int(i) for i in rng.permutation(8)[:5]]
    X[:, ga, :, :h] = 2 * rng.integers(-128, 129, (N, 16, h)); X[:, gb, :, :h] = 2 * rng.integers(-128, 129, (16, 1))
    for g in (ga, gb):
        X[:, g, :, h:] = 2 * rng.integers(-128, 128, (N, 16, W - h)) + 1
        C[:, g] = rng.integers(h, W, (N, 16, S)); C[:, g, 0] = rng.integers(0, h, (N, S))
    H[:, ga] = rng.integers(h, W, (N, 16, S)); H[:, gb] = rng.integers(0, h, (N, 16, S))
    X[:, gc] = (np.argsort(rng.random((16, 513)), axis=-1)[:, :N] - 256).T[:, :, None]; A[:, gc, ::2] = 255
    X[:, gd] = 2 * rng.integers(-128, 128, (16, 1))
    X[:, gd, 8:8 + m, v:h] += rng.integers(0, 2, (N, m, h - v)); X[:, gd, :8, h:] += rng.integers(0, 2, (N, 8, W - h))
    C[:, gd] = rng.integers(h, W, (N, 16, S)); C[:, gd, 0] = rng.integers(0, v, (N, S)); H[:, gd] = rng.integers(v, h, (N, 16, S))
    near = LIM + ((254 + RO) & 3); b = 2 * rng.integers(-128, 128, (16, 1))
    X[:, ge, :, :h] = b; X[:, ge, :, h:] = b + 1; X[:, ge, :, h + v:] = b + (np.argsort(rng.random(16)) < near)[:, None]; X[:, ge, :, ::16] = b
    C[:, ge] = h + 2 * rng.integers(0, v // 2, (N, 16, S)) + 1
    H[:, ge] = N * rng.integers(0, h // N, (N, 16, S)) + np.arange(N)[:, None, None]
    As[:, ge, 0, :h] = h + v * (np.arange(h) % N == np.array(HEARER[RO - 2])[:, None]) + 2 * rng.integers(0, v // 2, (N, h)) + 1
    A[:, ge, ::2] = 255
    return pack(X, As, C, H, R, A)
def check_inputs(d):
    bad = []
    for name, lo, hi in (("x", -256, 256), ("assoc", 0, W - 1), ("ctx", 0, W - 1), ("cand", 0, W - 1), ("pref", 0, 15), ("fail0", 0, 255)):
        v = np.asarray(d[name]).astype(np.float64)
        if not (np.min(v) >= lo and np.max(v) <= hi): bad.append("range of " + name)
        if np.any(v != np.rint(v)): bad.append("whole numbers in " + name)
    if np.any(np.sort(np.asarray(d["pref"]).astype(np.int64).reshape(-1, 8, 16, S), axis=2) != np.arange(16)[:, None]): bad.append("permutations in pref")
    return bad
def pick(a, ix):
    return np.take_along_axis(a, ix.reshape(N, 8, 1, 16 * S), 3).reshape(N, 8, 16, 16, S)
def front(R, row, fail):
    old = np.take_along_axis(R, row[:, :, None, :], 2)
    moved = np.where(np.arange(16)[:, None] == row[:, :, None, :], 0, R + (R < old))
    return np.where(fail[:, :, None, :], moved, R)
def reference(x, assoc, ctx, cand, pref, fail0):
    X = x.astype(np.float32).astype(np.int16).reshape(N, 8, 16, W); As = assoc.astype(np.int64).reshape(N, 8, 16, W)
    C = ctx.astype(np.int64).reshape(N, 8, 16, S); H = cand.astype(np.int64).reshape(N, 8, 16, S); R = pref.astype(np.int64).reshape(N, 8, 16, S); A = fail0.astype(np.int64).reshape(N, 8, S)
    for t in range(RO):
        q = np.array(HEARER[t]); sp = np.argsort(q)
        xk = pick(X, C); x0 = xk[:, :, :, 0]
        first = np.min(np.where(xk != x0[:, :, :, None], R[:, :, :, None], 16), axis=2)
        desc = np.any(R[:, :, :, None] == first[:, :, None], axis=3)
        top = np.min(first, axis=2)
        yk = pick(X, H)[q]
        miss = np.sum((yk != x0[:, :, :, None]) & desc[:, :, :, None], axis=2)
        ks = np.argmin(miss, axis=2)
        n = np.take_along_axis(H[q], ks[:, :, None, :], 2)[:, :, 0]
        y = np.take_along_axis(yk, ks[:, :, None, None, :], 3)[:, :, :, 0]
        un = y != x0; fail = np.sum(un, axis=2) > LIM + (A & 3); row = np.argmin(np.where(un, R, 16), axis=2)
        A = A + fail
        R = front(R, row, fail); R = front(R, row[sp], fail[sp])
        cn = np.take_along_axis(As, n[:, :, None, :], 3); hn = np.take_along_axis(As, n[sp][:, :, None, :], 3)
        C = np.where((first == top[:, :, None]) & (first < 16), cn, C); C[:, :, 0] = cn[:, :, 0]
        H = np.where(miss[sp] > 0, hn, H)
        if t < RO - 1:
            put = np.broadcast_to((16 * np.arange(S) + ks[sp])[:, :, None, :], (N, 8, 16, S))
            np.put_along_axis(X, put, np.where(desc, x0, y)[sp], 3)
    return {"yctx": C.reshape(N, 128, S).astype(np.float32), "ycand": H.reshape(N, 128, S).astype(np.float32), "ypref": R.reshape(N, 128, S).astype(np.float32), "yfail": A.astype(np.float32)}

@@ -1,0 +1,590 @@
+import math
+import numpy as np
+from concourse.mybir import AluOpType as A, ActivationFunctionType as F
+
+RO = 3
+S = 192
+WID = [128, 64]
+LO = [0, 128]
+NC = 2
+H0 = 64
+
+SCRATCH = {
+    "ps": ("psum", [128, 4096], "float32"),
+    "xs": ("sbuf", [128, 4096], "bfloat16"),
+    "az": ("sbuf", [128, 4096], "int32"),
+    "ci": ("sbuf", [128, S], "int32"), "hi": ("sbuf", [128, S], "int32"), "ri": ("sbuf", [128, S], "int32"),
+    "fi": ("sbuf", [8, S], "int32"), "fb": ("sbuf", [8, S], "bfloat16"),
+    "cf": ("sbuf", [128, S], "float32"), "cu": ("sbuf", [128, S], "uint16"),
+    "hf": ("sbuf", [128, S], "float32"), "hu": ("sbuf", [128, S], "uint16"), "hm16": ("sbuf", [128, S], "float16"),
+    "rb": ("sbuf", [128, S], "bfloat16"), "rb2": ("sbuf", [128, S], "bfloat16"), "rout": ("sbuf", [128, S], "float32"),
+    "a32": ("sbuf", [128, S], "int32"), "a3": ("sbuf", [128, S], "int32"), "aout": ("sbuf", [128, S], "float32"),
+    "p1": ("sbuf", [128, S], "bfloat16"), "t1": ("sbuf", [128, S], "bfloat16"),
+    "p2": ("sbuf", [128, S], "bfloat16"), "t2": ("sbuf", [128, S], "bfloat16"),
+    "ones": ("sbuf", [128, 128], "bfloat16"), "idn": ("sbuf", [128, 128], "bfloat16"), "bo0": ("sbuf", [128, 128], "bfloat16"),
+    "bo": ("sbuf", [128, 128], "bfloat16"), "k8a": ("sbuf", [8, 128], "bfloat16"), "k8": ("sbuf", [8, 128], "bfloat16"),
+    "mtmp": ("sbuf", [128, 384], "bfloat16"), "m1": ("sbuf", [128, 128], "bfloat16"), "m2": ("sbuf", [128, 128], "bfloat16"),
+    "m3": ("sbuf", [128, 128], "bfloat16"), "nb": ("sbuf", [128, 128], "bfloat16"), "ni": ("sbuf", [128, 128], "bfloat16"),
+    "ibig": ("sbuf", [128, 128], "bfloat16"), "i16": ("sbuf", [128, 128], "float16"),
+    "ek": ("sbuf", [128, 2048], "bfloat16"), "ek16": ("sbuf", [128, 2048], "float16"),
+    "pi": ("sbuf", [128, 1], "int32"), "ki": ("sbuf", [128, 1], "int32"), "kc": ("sbuf", [128, 1], "float32"),
+    "k16": ("sbuf", [128, 1], "float32"), "bk": ("sbuf", [128, 1], "float32"), "tc": ("sbuf", [128, 1], "float32"),
+    "rowq": ("sbuf", [128, 12], "float32"),
+}
+SEMAPHORES = ["sv", "ss", "sp", "sg", "lctx", "lcand", "lpref", "lfail", "lx", "las", "loc", "o0", "o1", "o2", "o3"]
+for _c in range(NC):
+    _w = WID[_c]
+    for _n, _k, _d in (("xg", 16, "bfloat16"), ("yg", 16, "bfloat16"), ("z", 16, "bfloat16"), ("yr", 16, "bfloat16"), ("e", 16, "bfloat16"),
+                       ("fk", 1, "bfloat16"), ("mk", 1, "float32"), ("km", 1, "float32"), ("ck", 1, "float32"), ("ct", 1, "float32"),
+                       ("wk", 1, "bfloat16"), ("ow", 1, "float16"), ("pr", 2, "float16"), ("hm", 1, "float32"), ("hd", 1, "float32"),
+                       ("ys", 1, "bfloat16"), ("un", 1, "bfloat16"), ("zf", 1, "bfloat16"), ("tt", 1, "float32"), ("de", 1, "bfloat16"),
+                       ("na", 1, "bfloat16"), ("nx", 1, "bfloat16")):
+        SCRATCH["%s%d" % (_n, _c)] = ("sbuf", [128, _k * _w], _d)
+    SCRATCH["cs%d" % _c] = ("sbuf", [128, _w // 8], "float16")
+    for _t in range(RO):
+        SCRATCH["sM%d%d" % (_t, _c)] = ("sbuf", [128, 2 * _w], "bfloat16")
+        SCRATCH["rM%d%d" % (_t, _c)] = ("sbuf", [128, 2 * _w], "bfloat16")
+        SCRATCH["L%d%d" % (_t, _c)] = ("sbuf", [128, _w // 8], "uint16")
+        SCRATCH["rL%d%d" % (_t, _c)] = ("sbuf", [128, _w // 16], "uint16")
+        SEMAPHORES += ["msg%d%d" % (_t, _c), "lst%d%d" % (_t, _c)]
+for _t in range(RO):
+    SCRATCH["sP%d" % _t] = ("sbuf", [128, S], "bfloat16")
+    SCRATCH["rP%d" % _t] = ("sbuf", [128, S], "bfloat16")
+    SCRATCH["sW%d" % _t] = ("sbuf", [128, 2 * S], "bfloat16")
+    SCRATCH["rW%d" % _t] = ("sbuf", [128, 2 * S], "bfloat16")
+    SEMAPHORES += ["wth%d" % _t, "phi%d" % _t]
+
+QS = {"V": "sv", "S": "ss", "P": "sp", "G": "sg"}
+LNB = 0.96 * math.log(2.0)
+
+
+def tracker(g, T):
+    qq = {"V": g.vector, "S": g.scalar, "P": g.tensor, "G": g, "Y": g.sync}
+    seen = {q: {} for q in qq}
+    know = {}
+    cnt = {q: 0 for q in QS}
+    lastw, readers, bank = {}, {}, {}
+
+    def need(q, tok):
+        s, n = tok
+        if seen[q].get(s, 0) >= n:
+            return
+        qq[q].wait_ge(T.sem[s], n)
+        for k, v in list(know.get(tok, {}).items()) + [(s, n)]:
+            if seen[q].get(k, 0) < v:
+                seen[q][k] = v
+
+    def before(q, r, w, b):
+        toks = {}
+        for k in r:
+            if k in lastw:
+                s, n = lastw[k]
+                toks[s] = max(toks.get(s, 0), n)
+        for k in w:
+            for s, n in ([lastw[k]] if k in lastw else []) + readers.get(k, []):
+                toks[s] = max(toks.get(s, 0), n)
+        for k in b:
+            for q2, (s, n) in bank.get(k, {}).items():
+                if q2 != q:
+                    toks[s] = max(toks.get(s, 0), n)
+        own = QS.get(q)
+        for s in sorted(toks, key=lambda s: s == own):
+            need(q, (s, toks[s]))
+
+    def after(q, tok, r, w, b):
+        know[tok] = dict(seen[q])
+        for k in r:
+            readers.setdefault(k, []).append(tok)
+        for k in w:
+            lastw[k] = tok
+            readers[k] = []
+        for k in b:
+            bank.setdefault(k, {})[q] = tok
+
+    def op(q, call, r=(), w=(), b=()):
+        before(q, r, w, b)
+        ins = call(qq[q])
+        cnt[q] += 1
+        ins.then_inc(T.sem[QS[q]], 1)
+        after(q, (QS[q], cnt[q]), r, w, b)
+
+    def mm(seq, r, w, b):
+        before("P", r, w, b)
+        ins = None
+        for out, lhsT, rhs, start, stop in seq:
+            ins = g.tensor.matmul(out, lhsT, rhs, start, stop)
+        cnt["P"] += 1
+        ins.then_inc(T.sem["sp"], 1)
+        after("P", ("sp", cnt["P"]), r, w, b)
+
+    def dma(q, out, in_, sem, r=(), w=()):
+        before(q, r, w, ())
+        qq[q].dma_start(out, in_).then_inc(T.sem[sem], 16)
+        after(q, (sem, 16), r, w, ())
+
+    def mark(key, tok):
+        lastw[key] = tok
+
+    return {"op": op, "mm": mm, "dma": dma, "before": before, "need": need, "mark": mark, "cnt": cnt}
+
+
+def rank_program(g, core, T, topo):
+    rank = T.rank_of(core)
+    if rank is None:
+        return
+    K = tracker(g, T)
+    op, mm, dma = K["op"], K["mm"], K["dma"]
+    nloc = [0]
+
+    def V(call, r=(), w=(), b=()):
+        op("V", call, r, w, b)
+
+    def SC(call, r=(), w=(), b=()):
+        op("S", call, r, w, b)
+
+    def bank(i, lo, n, step=1):
+        return T.ps[:, 512 * i + lo:512 * i + lo + n:step]
+
+    def B(name, c):
+        return T["%s%d" % (name, c)]
+
+    def send(t, out, in_, sem, rk, wk):
+        peer = T.cores[rank ^ (1 << t)]
+        rid, pid = topo.addr(peer)[:2]
+        ne = len(topo.engines(core, peer))
+        K["before"]("G", rk, (), ())
+        g.remote_dma(out_ap=out, in_ap=in_, remote_sem=T.sem[sem], local_sem=T.sem["loc"], pid=pid, routing_id=rid,
+                     dma_engine_mask=topo.mask(core, peer))
+        nloc[0] += ne
+        for k in wk:
+            K["mark"](k, (sem, ne))
+
+    def sl(c):
+        return slice(LO[c], LO[c] + WID[c])
+
+    def qr(c, a):
+        return slice(4 * WID[c] * a, 4 * WID[c] * (a + 1))
+
+    def qj(c, a, j):
+        return slice(4 * WID[c] * a + j, 4 * WID[c] * (a + 1), 4)
+
+    dma("S", T.ci[:], T.ctx[:], "lctx", (), ["ci"])
+    dma("Y", T.xs[:], T.x[:], "lx", (), ["xs"])
+    dma("S", T.ri[:], T.pref[:], "lpref", (), ["ri"])
+    dma("S", T.hi[:], T.cand[:], "lcand", (), ["hi"])
+    dma("S", T.fi[:], T.fail0[:], "lfail", (), ["fi"])
+    dma("Y", T.az[:], T.assoc[:], "las", ["xs"], ["az"])
+    V(lambda v: v.memset(T.ones[:], 1.0), (), ["ones"])
+    op("G", lambda e: e.affine_select(T.bo0[:], T.ones[:], [[-16, 8], [0, 16]], A.is_ge, 0.0, 0, 1), ["ones"], ["bo0"])
+    op("G", lambda e: e.affine_select(T.bo[:], T.bo0[:], [[16, 8], [0, 16]], A.is_ge, 0.0, 15, -1), ["bo0"], ["bo"])
+    op("G", lambda e: e.affine_select(T.idn[:], T.ones[:], [[-1, 128]], A.is_equal, 0.0, 0, 1), ["ones"], ["idn"])
+    op("G", lambda e: e.affine_select(T.k8a[:], T.ones[0:8, :], [[1, 128]], A.is_ge, 0.0, 0, -16), ["ones"], ["k8a"])
+    op("G", lambda e: e.affine_select(T.k8[:], T.k8a[:], [[-1, 128]], A.is_ge, 0.0, 15, 16), ["k8a"], ["k8"])
+    op("G", lambda e: e.iota(T.pi[:], [[1, 1]], 0, 1), (), ["pi"])
+    op("G", lambda e: e.iota(T.rowq[:], [[256, 12]], 0, 0, allow_small_or_imprecise_dtypes=True), (), ["rowq"])
+    SC(lambda s: s.activation(T.mtmp[:, 0:128], T.idn[:], F.Copy, scale=2.0), ["idn"], ["mt0"])
+    SC(lambda s: s.activation(T.mtmp[:, 128:256], T.idn[:], F.Copy, scale=16.0), ["idn"], ["mt1"])
+    SC(lambda s: s.activation(T.mtmp[:, 256:384], T.bo[:], F.Copy, scale=0.41), ["bo"], ["mt2"])
+    SC(lambda s: s.activation(T.nb[:], T.bo[:], F.Copy, scale=-1.0), ["bo"], ["nb"])
+    SC(lambda s: s.activation(T.ni[:], T.idn[:], F.Copy, scale=-1.0), ["idn"], ["ni"])
+    SC(lambda s: s.activation(T.ibig[:], T.idn[:], F.Copy, scale=1024.0), ["idn"], ["ibig"])
+    V(lambda v: v.memset(T.ek[:], 0.0), (), ["ek"])
+    for k in range(16):
+        V(lambda v: v.tensor_copy(T.ek[:, 129 * k:129 * k + 113:16], T.bo[:, 0:128:16]), ["bo", "ek"], ["ek_%d" % k])
+    ekk = ["ek_%d" % k for k in range(16)]
+    V(lambda v: v.tensor_tensor(T.m1[:], T.mtmp[:, 0:128], T.bo[:], A.subtract), ["mt0", "bo"], ["m1"])
+    V(lambda v: v.tensor_scalar(T.ki[:], T.pi[:], 15, None, A.bitwise_and), ["pi"], ["ki"])
+    V(lambda v: v.tensor_copy(T.kc[:], T.ki[:]), ["ki"], ["kc"])
+    V(lambda v: v.tensor_copy(T.cu[:], T.ci[:]), ["ci"], ["cu0", "cu1"])
+
+    def orders():
+        V(lambda v: v.tensor_copy(T.rb[:], T.ri[:]), ["ri"], ["rb"])
+        SC(lambda s: s.activation(T.sW0[:, 0:S], T.rb[:], F.Exp, scale=-5.0 * math.log(2.0)), ["rb"], ["w0"])
+
+    def counts():
+        V(lambda v: v.tensor_copy(T.fb[:], T.fi[:]), ["fi"], ["fb"])
+        mm([(bank(7, 0, S), T.k8[:], T.fb[:], True, True)], ["k8", "fb"], ["A0"], [7])
+        V(lambda v: v.tensor_copy(T.hu[:], T.hi[:]), ["hi"], ["hu0", "hu1"])
+        V(lambda v: v.tensor_copy(T.a32[:], bank(7, 0, S)), ["A0"], ["a32"], [7])
+
+    def late_constants():
+        V(lambda v: v.tensor_tensor(T.m2[:], T.mtmp[:, 128:256], T.bo[:], A.subtract), ["mt1", "bo"], ["m2"])
+        V(lambda v: v.tensor_tensor(T.m3[:], T.idn[:], T.mtmp[:, 256:384], A.subtract), ["mt2", "idn"], ["m3"])
+        V(lambda v: v.tensor_copy(T.i16[:], T.idn[:]), ["idn"], ["i16"])
+        V(lambda v: v.tensor_copy(T.ek16[:], T.ek[:]), ekk, ["ek16"])
+        V(lambda v: v.tensor_scalar(T.k16[:], T.kc[:], 16.0, None, A.mult), ["kc"], ["k16"])
+        V(lambda v: v.tensor_scalar(T.bk[:], T.kc[:], -LNB, 84.5, A.mult, A.add), ["kc"], ["bk"])
+        V(lambda v: v.tensor_scalar(T.tc[:], T.kc[:], 0.0, -1e29, A.is_equal, A.mult), ["kc"], ["tc"])
+        for c in range(NC):
+            n, o = WID[c] // 16, LO[c] // 16
+            V(lambda v: v.tensor_scalar(B("cs", c)[:, 0:n], T.rowq[:, 0:n], 0.0, 2048.0, A.mult, A.add), ["rowq"], ["csa%d" % c])
+            V(lambda v: v.tensor_scalar(B("cs", c)[:, n:2 * n], T.rowq[:, o:o + n], T.k16[:], None, A.add), ["rowq", "k16"], ["csb%d" % c])
+        V(lambda v: v.tensor_copy(T.cf[:], T.ci[:]), ["ci"], ["cf0", "cf1"])
+        V(lambda v: v.tensor_copy(T.hf[:], T.hi[:]), ["hi"], ["hf0", "hf1"])
+        V(lambda v: v.tensor_scalar(T.hm16[:], T.hi[:], -2048.0, None, A.add), ["hi"], ["hm160", "hm161"])
+
+    def ek(k):
+        return T.ek[:, 128 * k:128 * k + 128]
+
+    def ek16(k):
+        return T.ek16[:, 128 * k:128 * k + 128]
+
+    def pieces(c):
+        return list(range(WID[c] // H0))
+
+    def gather(q, which, c, p):
+        name, lst = (("xg", T.cu), ("yg", T.hu))[which]
+        lkey = ("cu%d", "hu%d")[which] % c
+        dst = B(name, c)[:, 16 * H0 * p:16 * H0 * (p + 1)]
+        src = T.xs[:, :].indirect(lst[:, LO[c] + H0 * p:LO[c] + H0 * (p + 1)])
+        key = "%s%d_%d" % (name, c, p)
+        if q == "V":
+            V(lambda v: v.tensor_copy(dst, src), [lkey, "xs"], [key])
+        else:
+            SC(lambda s: s.activation(dst, src, F.Copy), [lkey, "xs"], [key])
+
+    def gx(q, c, p):
+        gather(q, 0, c, p)
+
+    def gy(q, c, p):
+        gather(q, 1, c, p)
+
+    def gk(name, c):
+        return ["%s%d_%d" % (name, c, p) for p in pieces(c)]
+
+    def thr(t):
+        sw = B("sW", t)
+        V(lambda v: v.tensor_scalar(T.a3[:], T.a32[:], 3, None, A.bitwise_and), ["a32"], ["a3"])
+        V(lambda v: v.tensor_scalar(sw[:, S:2 * S], T.a3[:], 5.5, None, A.add), ["a3"], ["thr%d" % t])
+        send(t, B("rW", t)[:], sw[:], "wth%d" % t, ["w%d" % t, "thr%d" % t], ["rw%d" % t])
+
+    def x0dup(c):
+        mm([(bank(c, j, 4 * WID[c], 4), T.idn[:], B("xg", c)[:, 0:16 * WID[c]:16], True, True) for j in range(4)],
+           ["idn"] + gk("xg", c), ["x0d%d" % c], [c])
+
+    def wdb(c):
+        return ((2, 0), (1, 256))[c]
+
+    def wdup(t, c):
+        b, o = wdb(c)
+        mm([(bank(b, o + j, 4 * WID[c] - j, 4), T.idn[:], B("sW", t)[:, sl(c)], True, True) for j in range(4)],
+           ["idn", "w%d" % t], ["wd%d" % c], [b])
+
+    def x0copy(t, c):
+        V(lambda v: v.tensor_copy(T["sM%d%d" % (t, c)][:, 0:WID[c]], B("xg", c)[:, 0:16 * WID[c]:16]), gk("xg", c), ["sx%d%d" % (t, c)])
+
+    def spk_cmp(c, a):
+        V(lambda v: v.tensor_tensor(B("z", c)[:, qr(c, a)], B("xg", c)[:, a:16 * WID[c]:4], bank(c, 0, 4 * WID[c]), A.not_equal),
+          gk("xg", c) + ["x0d%d" % c], ["z%d%d" % (c, a)], [c])
+
+    def spk_wt(c, a):
+        z = B("z", c)[:, qr(c, a)]
+        b, o = wdb(c)
+        V(lambda v: v.tensor_tensor(z, z, bank(b, o, 4 * WID[c]), A.mult), ["wd%d" % c], ["z%d%d" % (c, a)], [b])
+
+    def spk_y(c, a):
+        bb = 3 + a % 2
+        mm([(bank(bb, 0, 4 * WID[c]), T.m1[:], B("z", c)[:, qr(c, a)], True, True)], ["m1", "z%d%d" % (c, a)], ["Y%d" % bb], [bb])
+
+    def spk_relu(c, a):
+        bb = 3 + a % 2
+        SC(lambda s: s.activation(B("yr", c)[:, qr(c, a)], bank(bb, 0, 4 * WID[c]), F.Relu), ["Y%d" % bb], ["yr%d%d" % (c, a)], [bb])
+
+    def spk_sum(c, a):
+        seq = [(bank(5, 0, WID[c]), T.idn[:], B("yr", c)[:, qj(c, a, j)], a + j == 0, a + j == 6) for j in range(4)]
+        mm(seq, ["idn", "yr%d%d" % (c, a)], ["dsum"], [5])
+
+    def spk_nd(t, c):
+        sm, w = T["sM%d%d" % (t, c)], WID[c]
+        SC(lambda s: s.activation(sm[:, w:2 * w], bank(5, 0, w), F.Relu, bias=1.0, scale=-float(2.0 ** 80)), ["dsum"], ["nd%d%d" % (t, c)], [5])
+        send(t, T["rM%d%d" % (t, c)][:], sm[:], "msg%d%d" % (t, c), ["sx%d%d" % (t, c), "nd%d%d" % (t, c)], ["rm%d%d" % (t, c)])
+
+    def mask1(c):
+        w = WID[c]
+        seq = [(bank(5, 128, w), ek(a + 4 * j), B("z", c)[:, qj(c, a, j)], a + j == 0, a + j == 6) for a in range(4) for j in range(4)]
+        mm(seq, ekk + ["z%d%d" % (c, a) for a in range(4)], ["F"], [5])
+        SC(lambda s: s.activation(B("fk", c)[:], bank(5, 128, w), F.Copy), ["F"], ["fk%d" % c], [5])
+
+    def mask2(c):
+        w = WID[c]
+        mm([(bank(5, 256, w), T.m2[:], B("fk", c)[:], True, True)], ["m2", "fk%d" % c], ["mp"], [5])
+        V(lambda v: v.tensor_scalar(B("mk", c)[:], bank(5, 256, w), T.tc[:], None, A.is_gt), ["mp", "tc"], ["mk%d" % c], [5])
+
+    def mask3(c):
+        SC(lambda s: s.activation(B("km", c)[:], B("mk", c)[:], F.Copy, bias=1.0, scale=-1.0), ["mk%d" % c], ["km%d" % c])
+        V(lambda v: v.tensor_tensor(B("ck", c)[:], T.cf[:, sl(c)], B("km", c)[:], A.mult), ["cf%d" % c, "km%d" % c], ["ck%d" % c])
+
+    def xb(c):
+        return 2 + c
+
+    def hb(c):
+        return 7 - c
+
+    def hear_in(t, c):
+        rm, w = T["rM%d%d" % (t, c)], WID[c]
+        seq = []
+        for j in range(4):
+            seq.append((bank(xb(c), j, 4 * w, 4), T.idn[:], rm[:, 0:w], True, False))
+            seq.append((bank(xb(c), j, 4 * w, 4), T.ibig[:], rm[:, w:2 * w], False, True))
+        mm(seq, ["idn", "ibig", "rm%d%d" % (t, c)], ["xm%d" % c], [xb(c)])
+
+    def hear_pre(t, c):
+        rm, w = T["rM%d%d" % (t, c)], WID[c]
+        mm([(bank(c, 0, w), T.idn[:], rm[:, 0:w], True, True),
+            (bank(c, w, w), T.idn[:], B("rW", t)[:, sl(c)], True, True)],
+           ["idn", "rm%d%d" % (t, c), "rw%d" % t], ["pre%d" % c], [c])
+        if t < RO - 1:
+            SC(lambda s: s.activation(B("de", c)[:], rm[:, w:2 * w], F.Copy, bias=1.0, scale=-1.0), ["rm%d%d" % (t, c)], ["de%d" % c])
+            V(lambda v: v.tensor_tensor(B("nx", c)[:], B("de", c)[:], bank(c, 0, w), A.mult), ["de%d" % c, "pre%d" % c], ["nx%d" % c], [c])
+
+    def hear_cmp(c, a):
+        V(lambda v: v.tensor_tensor(B("e", c)[:, qr(c, a)], B("yg", c)[:, a:16 * WID[c]:4], bank(xb(c), 0, 4 * WID[c]), A.not_equal),
+          gk("yg", c) + ["xm%d" % c], ["e%d%d" % (c, a)], [xb(c)])
+
+    def hear_cnt(t, c, a):
+        seq, w = [], WID[c]
+        if a == 0:
+            seq.append((bank(hb(c), 0, w), T.nb[:], T["rM%d%d" % (t, c)][:, w:2 * w], True, False))
+        for j in range(4):
+            seq.append((bank(hb(c), 0, w), ek(a + 4 * j), B("e", c)[:, qj(c, a, j)], False, a + j == 6))
+        mm(seq, ekk + ["nb", "rm%d%d" % (t, c), "e%d%d" % (c, a)], ["miss%d" % c], [hb(c)])
+
+    def pick1(t, c):
+        h, w = hb(c), WID[c]
+        SC(lambda s: s.activation(B("wk", c)[:], bank(h, 0, w), F.Exp, bias=T.bk[:], scale=-16.0 * LNB), ["miss%d" % c, "bk"], ["wk%d" % c], [h])
+        SC(lambda s: s.activation(B("hm", c)[:], bank(h, 0, w), F.Sign), ["miss%d" % c], ["hm%d" % c], [h])
+        mm([(bank(h, 128, w), T.m3[:], B("wk", c)[:], True, True)], ["m3", "wk%d" % c], ["G%d" % c], [h])
+
+    def pick2(t, c):
+        h, w = hb(c), WID[c]
+        pr, n = B("pr", c), WID[c] // 8
+        V(lambda v: v.tensor_scalar(B("ow", c)[:], bank(h, 128, w), 0.0, None, A.is_gt), ["G%d" % c], ["ow%d" % c], [h])
+        V(lambda v: v.tensor_scalar(pr[:, w:2 * w], bank(h, 128, w), 0.0, T.kc[:], A.is_gt, A.mult), ["G%d" % c, "kc"], ["prq%d" % c], [h])
+        V(lambda v: v.tensor_tensor(pr[:, 0:w], B("ow", c)[:], T.hm16[:, sl(c)], A.mult), ["ow%d" % c, "hm16%d" % c], ["prn%d" % c])
+        seq = [(bank(h, 256, n), T.i16[:], B("cs", c)[:], True, False)]
+        for k in range(16):
+            seq.append((bank(h, 256, n), ek16(k), pr[:, k:2 * w:16], False, k == 15))
+        mm(seq, ["i16", "csa%d" % c, "csb%d" % c, "ek16", "prq%d" % c, "prn%d" % c], ["lp%d" % c], [h])
+
+    def pick3(t, c):
+        h, n = hb(c), WID[c] // 16
+        lt = T["L%d%d" % (t, c)]
+        V(lambda v: v.tensor_copy(lt[:], bank(h, 256, 2 * n)), ["lp%d" % c], ["L%d" % c], [h])
+        send(t, T["rL%d%d" % (t, c)][:], lt[:, 0:n], "lst%d%d" % (t, c), ["L%d" % c], ["rl%d%d" % (t, c)])
+
+    def post_h(t, c):
+        hf, n = T.hf[:, sl(c)], WID[c] // 16
+        lt = T["L%d%d" % (t, c)]
+        hd = B("hd", c)
+        V(lambda v: v.tensor_tensor(hd[:], T.az[:, :].indirect(lt[:, 0:n]), hf, A.subtract), ["az", "L%d" % c, "hf%d" % c], ["hd%d" % c])
+        V(lambda v: v.tensor_tensor(hd[:], hd[:], B("hm", c)[:], A.mult), ["hm%d" % c], ["hd%d" % c])
+        V(lambda v: v.tensor_tensor(hf, hf, hd[:], A.add), ["hd%d" % c], ["hf%d" % c])
+        if t < RO - 1:
+            V(lambda v: v.tensor_copy(T.hu[:, sl(c)], hf), ["hf%d" % c], ["hu%d" % c])
+            V(lambda v: v.tensor_scalar(T.hm16[:, sl(c)], hf, -2048.0, None, A.add), ["hf%d" % c], ["hm16%d" % c])
+
+    def post_y(t, c):
+        lt, n = T["L%d%d" % (t, c)], WID[c] // 16
+        SC(lambda s: s.activation(B("ys", c)[:], T.xs[:, :].indirect(lt[:, 0:n]), F.Copy), ["xs", "L%d" % c], ["ys%d" % c])
+
+    def post_na(t, c):
+        lt, n, w = T["L%d%d" % (t, c)], WID[c] // 16, WID[c]
+        V(lambda v: v.tensor_tensor(B("na", c)[:], T.xs[:, :].indirect(lt[:, 0:n]), T["rM%d%d" % (t, c)][:, w:2 * w], A.mult),
+          ["xs", "L%d" % c, "rm%d%d" % (t, c)], ["na%d" % c])
+
+    def post_un(t, c):
+        w = WID[c]
+        V(lambda v: v.tensor_tensor(B("un", c)[:], B("ys", c)[:], bank(c, 0, w), A.not_equal), ["ys%d" % c, "pre%d" % c], ["un%d" % c], [c])
+        V(lambda v: v.tensor_tensor(B("zf", c)[:], B("un", c)[:], bank(c, w, w), A.mult), ["un%d" % c, "pre%d" % c], ["zf%d" % c], [c])
+        mm([(bank(4, 0, w), T.bo[:], B("un", c)[:], True, True), (bank(4, 128, w), T.m1[:], B("zf", c)[:], True, True)],
+           ["bo", "m1", "un%d" % c, "zf%d" % c], ["UY"], [4])
+
+    def post_phi(t, c):
+        w = WID[c]
+        V(lambda v: v.tensor_tensor(B("tt", c)[:], bank(4, 0, w), B("rW", t)[:, S + LO[c]:S + LO[c] + w], A.is_le), ["UY", "rw%d" % t], ["tt%d" % c], [4])
+        V(lambda v: v.tensor_tensor(B("sP", t)[:, sl(c)], bank(4, 128, w), B("tt", c)[:], A.is_gt), ["UY", "tt%d" % c], ["sp%d%d" % (t, c)], [4])
+
+    def send_phi(t):
+        send(t, B("rP", t)[:], B("sP", t)[:], "phi%d" % t, ["sp%d%d" % (t, c) for c in range(NC)], ["rp%d" % t])
+
+    def scatter(t, c):
+        lt, n = T["L%d%d" % (t, c)], WID[c] // 16
+        V(lambda v: v.tensor_tensor(T.xs[:, :].indirect(lt[:, n:2 * n]), B("na", c)[:], B("nx", c)[:], A.add),
+          ["L%d" % c, "na%d" % c, "nx%d" % c], ["xs"])
+
+    def cupd(t, c):
+        V(lambda v: v.tensor_tensor(B("ct", c)[:], T.az[:, :].indirect(T["rL%d%d" % (t, c)][:]), B("mk", c)[:], A.mult),
+          ["az", "rl%d%d" % (t, c), "mk%d" % c], ["ct%d" % c])
+        V(lambda v: v.tensor_tensor(T.cf[:, sl(c)], B("ct", c)[:], B("ck", c)[:], A.add), ["ct%d" % c, "ck%d" % c], ["cf%d" % c])
+        if t < RO - 1:
+            V(lambda v: v.tensor_copy(T.cu[:, sl(c)], T.cf[:, sl(c)]), ["cf%d" % c], ["cu%d" % c])
+
+    def move1(phi, pk, rb, rk, pb):
+        V(lambda v: v.tensor_tensor(pb[:], phi[:], rb[:], A.mult), [rk] + pk, [pb.name])
+        mm([(bank(3, 0, S), T.bo[:], pb[:], True, True)], ["bo", pb.name], ["rf"], [3])
+        mm([(bank(4, 0, S), T.idn[:], rb[:], True, False), (bank(4, 0, S), T.ni[:], pb[:], False, False)], ["idn", "ni", rk, pb.name], ["RR"], [4])
+
+    def move2(rb, rk, tb):
+        V(lambda v: v.tensor_tensor(tb[:], bank(3, 0, S), rb[:], A.is_gt), ["rf", rk], [tb.name], [3])
+        mm([(bank(4, 0, S), T.idn[:], tb[:], False, True)], ["idn", tb.name], ["RR"], [4])
+
+    def rup1(t):
+        move1(B("rP", t), ["rp%d" % t], T.rb, "rb", T.p1)
+        mm([(bank(5, 0, S), T.bo[:], B("rP", t)[:], True, True)], ["bo", "rp%d" % t], ["Fo"], [5])
+
+    def rup2(t):
+        move2(T.rb, "rb", T.t1)
+
+    def rup3(t):
+        V(lambda v: v.tensor_copy(T.rb2[:], bank(4, 0, S)), ["RR"], ["rb2"], [4])
+        move1(B("sP", t), ["sp%d%d" % (t, c) for c in range(NC)], T.rb2, "rb2", T.p2)
+
+    def rup4(t):
+        move2(T.rb2, "rb2", T.t2)
+        if t < RO - 1:
+            SC(lambda s: s.activation(B("sW", t + 1)[:, 0:S], bank(4, 0, S), F.Exp, scale=-5.0 * math.log(2.0)), ["RR"], ["w%d" % (t + 1)], [4])
+        else:
+            V(lambda v: v.tensor_copy(T.rout[:], bank(4, 0, S)), ["RR"], ["rout"], [4])
+            dma("Y", T.ypref[:], T.rout[:], "o2", ["rout"], [])
+
+    def rup5(t):
+        V(lambda v: v.tensor_copy(T.rb[:], bank(4, 0, S)), ["RR"], ["rb"], [4])
+
+    def aup(t):
+        if t < RO - 1:
+            V(lambda v: v.tensor_tensor(T.a32[:], bank(5, 0, S), T.a32[:], A.add), ["Fo"], ["a32"], [5])
+        else:
+            V(lambda v: v.tensor_tensor(T.aout[:], bank(5, 0, S), T.a32[:], A.add), ["Fo", "a32"], ["aout"], [5])
+            dma("S", T.yfail[:], T.aout[0:128:16, :], "o3", ["aout"], [])
+
+    for t in range(RO):
+        if t == 0:
+            gx("S", 0, 0)
+            gx("V", 0, 1)
+            x0dup(0)
+            orders()
+            gx("S", 1, 0)
+            wdup(t, 0)
+            for a in range(4):
+                spk_cmp(0, a)
+            counts()
+            x0dup(1)
+            wdup(t, 1)
+            thr(t)
+        else:
+            x0dup(0)
+            for a in range(4):
+                spk_cmp(0, a)
+                if a == 0:
+                    cupd(t - 1, 1)
+                    gx("S", 1, 0)
+            rup1(t - 1)
+            gy("S", 0, 0)
+            x0copy(t, 0)
+            rup2(t - 1)
+            x0dup(1)
+            spk_cmp(1, 0)
+            rup3(t - 1)
+            spk_cmp(1, 1)
+            rup4(t - 1)
+            wdup(t, 0)
+            spk_cmp(1, 2)
+            spk_cmp(1, 3)
+            wdup(t, 1)
+            rup5(t - 1)
+            aup(t - 1)
+            thr(t)
+        if t == 0:
+            x0copy(t, 0)
+        for a in range(4):
+            spk_wt(0, a)
+            spk_y(0, a)
+            spk_relu(0, a)
+            if a > 0:
+                spk_sum(0, a - 1)
+        x0copy(t, 1)
+        if t == 0:
+            spk_cmp(1, 0)
+        spk_wt(1, 0)
+        spk_sum(0, 3)
+        spk_nd(t, 0)
+        for a in range(4):
+            if a:
+                if t == 0:
+                    spk_cmp(1, a)
+                spk_wt(1, a)
+            spk_y(1, a)
+            spk_relu(1, a)
+            if a:
+                spk_sum(1, a - 1)
+        spk_sum(1, 3)
+        spk_nd(t, 1)
+        if t == 0:
+            late_constants()
+            gy("V", 0, 0)
+            gy("S", 0, 1)
+        else:
+            gy("V", 1, 0)
+            gy("S", 0, 1)
+        mask1(0)
+        mask2(0)
+        mask1(1)
+        mask2(1)
+        if t == 0:
+            gy("S", 1, 0)
+        hear_in(t, 0)
+        for a in range(4):
+            hear_cmp(0, a)
+            hear_cnt(t, 0, a)
+        pick1(t, 0)
+        mask3(0)
+        mask3(1)
+        hear_pre(t, 0)
+        pick2(t, 0)
+        hear_in(t, 1)
+        hear_cmp(1, 0)
+        hear_cnt(t, 1, 0)
+        hear_cmp(1, 1)
+        hear_cnt(t, 1, 1)
+        pick3(t, 0)
+        post_y(t, 0)
+        for a in (2, 3):
+            hear_cmp(1, a)
+            hear_cnt(t, 1, a)
+        pick1(t, 1)
+        hear_pre(t, 1)
+        post_h(t, 0)
+        pick2(t, 1)
+        post_un(t, 0)
+        pick3(t, 1)
+        post_y(t, 1)
+        if t < RO - 1:
+            post_na(t, 0)
+            post_na(t, 1)
+            scatter(t, 0)
+            scatter(t, 1)
+        post_phi(t, 0)
+        post_un(t, 1)
+        if t < RO - 1:
+            post_h(t, 1)
+        post_phi(t, 1)
+        send_phi(t)
+        if t == RO - 1:
+            post_h(t, 1)
+            dma("Y", T.ycand[:], T.hf[:], "o1", ["hf0", "hf1"], [])
+        cupd(t, 0)
+        if t < RO - 1:
+            gx("V", 0, 0)
+            gx("S", 0, 1)
+    cupd(RO - 1, 1)
+    dma("Y", T.yctx[:], T.cf[:], "o0", ["cf0", "cf1"], [])
+    rup1(RO - 1)
+    rup2(RO - 1)
+    rup3(RO - 1)
+    rup4(RO - 1)
+    aup(RO - 1)
+    for s in ("o0", "o1", "o2", "o3"):
+        g.sync.wait_ge(T.sem[s], 16)
+    for q in ("V", "S", "P", "G"):
+        K["need"]("G", (QS[q], K["cnt"][q]))
+    g.wait_ge(T.sem["loc"], nloc[0])

@@ -20,7 +20,6 @@ SCRATCH = {
     "rb": ("sbuf", [128, S], "bfloat16"), "rb2": ("sbuf", [128, S], "bfloat16"), "rout": ("sbuf", [128, S], "float32"),
     "a32": ("sbuf", [128, S], "int32"), "a3": ("sbuf", [128, S], "int32"), "aout": ("sbuf", [128, S], "float32"),
     "p1": ("sbuf", [128, S], "bfloat16"), "t1": ("sbuf", [128, S], "bfloat16"),
-    "p2": ("sbuf", [128, S], "bfloat16"), "t2": ("sbuf", [128, S], "bfloat16"),
     "ones": ("sbuf", [128, 128], "bfloat16"), "idn": ("sbuf", [128, 128], "bfloat16"), "bo0": ("sbuf", [128, 128], "bfloat16"),
     "bo": ("sbuf", [128, 128], "bfloat16"), "k8a": ("sbuf", [8, 128], "bfloat16"), "k8": ("sbuf", [8, 128], "bfloat16"),
     "mtmp": ("sbuf", [128, 384], "bfloat16"), "m1": ("sbuf", [128, 128], "bfloat16"), "m2": ("sbuf", [128, 128], "bfloat16"),
@@ -34,7 +33,7 @@ SCRATCH = {
 SEMAPHORES = ["sv", "ss", "sp", "sg", "lctx", "lcand", "lpref", "lfail", "lx", "las", "loc", "o0", "o1", "o2", "o3"]
 for _c in range(NC):
     _w = WID[_c]
-    for _n, _k, _d in (("xg", 16, "bfloat16"), ("yg", 16, "bfloat16"), ("z", 16, "bfloat16"), ("yr", 16, "bfloat16"), ("e", 16, "bfloat16"),
+    for _n, _k, _d in (("xg", 16, "bfloat16"), ("yg", 16, "bfloat16"), ("z", 16, "bfloat16"), ("yr", 16, "bfloat16"), ("nv", 1, "float32"), ("nd", 1, "bfloat16"),
                        ("fk", 1, "bfloat16"), ("mk", 1, "float32"), ("km", 1, "float32"), ("ck", 1, "float32"), ("ct", 1, "float32"),
                        ("wk", 1, "bfloat16"), ("ow", 1, "float16"), ("pr", 2, "float16"), ("hm", 1, "float32"), ("hd", 1, "float32"),
                        ("ys", 1, "bfloat16"), ("un", 1, "bfloat16"), ("zf", 1, "bfloat16"), ("tt", 1, "float32"), ("de", 1, "bfloat16"),
@@ -42,8 +41,8 @@ for _c in range(NC):
         SCRATCH["%s%d" % (_n, _c)] = ("sbuf", [128, _k * _w], _d)
     SCRATCH["cs%d" % _c] = ("sbuf", [128, _w // 8], "float16")
     for _t in range(RO):
-        SCRATCH["sM%d%d" % (_t, _c)] = ("sbuf", [128, 2 * _w], "bfloat16")
-        SCRATCH["rM%d%d" % (_t, _c)] = ("sbuf", [128, 2 * _w], "bfloat16")
+        SCRATCH["sM%d%d" % (_t, _c)] = ("sbuf", [128, _w], "float16")
+        SCRATCH["rM%d%d" % (_t, _c)] = ("sbuf", [128, _w], "float16")
         SCRATCH["L%d%d" % (_t, _c)] = ("sbuf", [128, _w // 8], "uint16")
         SCRATCH["rL%d%d" % (_t, _c)] = ("sbuf", [128, _w // 16], "uint16")
         SEMAPHORES += ["msg%d%d" % (_t, _c), "lst%d%d" % (_t, _c)]
@@ -54,6 +53,7 @@ for _t in range(RO):
     SCRATCH["rW%d" % _t] = ("sbuf", [128, 2 * S], "bfloat16")
     SEMAPHORES += ["wth%d" % _t, "phi%d" % _t]
 
+OPT = {"sq": 0, "sqa": 0, "nda": 3, "mf": 0, "vr": 2, "cb": 2}
 QS = {"V": "sv", "S": "ss", "P": "sp", "G": "sg"}
 LNB = 0.96 * math.log(2.0)
 
@@ -187,7 +187,7 @@ def rank_program(g, core, T, topo):
     SC(lambda s: s.activation(T.mtmp[:, 256:384], T.bo[:], F.Copy, scale=0.41), ["bo"], ["mt2"])
     SC(lambda s: s.activation(T.nb[:], T.bo[:], F.Copy, scale=-1.0), ["bo"], ["nb"])
     SC(lambda s: s.activation(T.ni[:], T.idn[:], F.Copy, scale=-1.0), ["idn"], ["ni"])
-    SC(lambda s: s.activation(T.ibig[:], T.idn[:], F.Copy, scale=1024.0), ["idn"], ["ibig"])
+    SC(lambda s: s.activation(T.ibig[:], T.idn[:], F.Copy, scale=-1024.0), ["idn"], ["ibig"])
     V(lambda v: v.memset(T.ek[:], 0.0), (), ["ek"])
     for k in range(16):
         V(lambda v: v.tensor_copy(T.ek[:, 129 * k:129 * k + 113:16], T.bo[:, 0:128:16]), ["bo", "ek"], ["ek_%d" % k])
@@ -203,9 +203,9 @@ def rank_program(g, core, T, topo):
 
     def counts():
         V(lambda v: v.tensor_copy(T.fb[:], T.fi[:]), ["fi"], ["fb"])
-        mm([(bank(7, 0, S), T.k8[:], T.fb[:], True, True)], ["k8", "fb"], ["A0"], [7])
+        mm([(bank(5, 320, S), T.k8[:], T.fb[:], True, True)], ["k8", "fb"], ["A0"], [5])
         V(lambda v: v.tensor_copy(T.hu[:], T.hi[:]), ["hi"], ["hu0", "hu1"])
-        V(lambda v: v.tensor_copy(T.a32[:], bank(7, 0, S)), ["A0"], ["a32"], [7])
+        V(lambda v: v.tensor_copy(T.a32[:], bank(5, 320, S)), ["A0"], ["a32"], [5])
 
     def late_constants():
         V(lambda v: v.tensor_tensor(T.m2[:], T.mtmp[:, 128:256], T.bo[:], A.subtract), ["mt1", "bo"], ["m2"])
@@ -270,17 +270,29 @@ def rank_program(g, core, T, topo):
         mm([(bank(b, o + j, 4 * WID[c] - j, 4), T.idn[:], B("sW", t)[:, sl(c)], True, True) for j in range(4)],
            ["idn", "w%d" % t], ["wd%d" % c], [b])
 
-    def x0copy(t, c):
-        V(lambda v: v.tensor_copy(T["sM%d%d" % (t, c)][:, 0:WID[c]], B("xg", c)[:, 0:16 * WID[c]:16]), gk("xg", c), ["sx%d%d" % (t, c)])
-
     def spk_cmp(c, a):
         V(lambda v: v.tensor_tensor(B("z", c)[:, qr(c, a)], B("xg", c)[:, a:16 * WID[c]:4], bank(c, 0, 4 * WID[c]), A.not_equal),
           gk("xg", c) + ["x0d%d" % c], ["z%d%d" % (c, a)], [c])
 
+    def dif_b(a):
+        w, c = WID[1], 1
+        o = 4 * w * a
+        seq = [(bank(6, o, 4 * w), T.idn[:], B("xg", c)[:, a:16 * w:4], True, False)]
+        seq += [(bank(6, o + j, 4 * w - j, 4), T.ni[:], B("xg", c)[:, 0:16 * w:16], False, j == 3) for j in range(4)]
+        mm(seq, ["idn", "ni"] + gk("xg", c), ["dif%d" % a], [6 + a // 2])
+
+    def sqr_b():
+        w = WID[1]
+        SC(lambda s: s.activation(T.z1[:, 0:16 * w], bank(6, 0, 16 * w), F.Square), ["dif%d" % a for a in range(4)], ["z1%d" % a for a in range(4)], [6, 7])
+
+    def x0one():
+        w = WID[1]
+        mm([(bank(1, 0, w), T.idn[:], T.xg1[:, 0:16 * w:16], True, True)], ["idn"] + gk("xg", 1), ["x0d1"], [1])
+
     def spk_wt(c, a):
         z = B("z", c)[:, qr(c, a)]
         b, o = wdb(c)
-        V(lambda v: v.tensor_tensor(z, z, bank(b, o, 4 * WID[c]), A.mult), ["wd%d" % c], ["z%d%d" % (c, a)], [b])
+        V(lambda v: v.tensor_tensor(z, z, bank(b, o, 4 * WID[c]), A.min), ["wd%d" % c], ["z%d%d" % (c, a)], [b])
 
     def spk_y(c, a):
         bb = 3 + a % 2
@@ -288,27 +300,34 @@ def rank_program(g, core, T, topo):
 
     def spk_relu(c, a):
         bb = 3 + a % 2
+        if c == 1 and a >= OPT["vr"]:
+            V(lambda v: v.tensor_scalar(B("yr", c)[:, qr(c, a)], bank(bb, 0, 4 * WID[c]), 0.0, None, A.max), ["Y%d" % bb], ["yr%d%d" % (c, a)], [bb])
+            return
         SC(lambda s: s.activation(B("yr", c)[:, qr(c, a)], bank(bb, 0, 4 * WID[c]), F.Relu), ["Y%d" % bb], ["yr%d%d" % (c, a)], [bb])
 
     def spk_sum(c, a):
-        seq = [(bank(5, 0, WID[c]), T.idn[:], B("yr", c)[:, qj(c, a, j)], a + j == 0, a + j == 6) for j in range(4)]
-        mm(seq, ["idn", "yr%d%d" % (c, a)], ["dsum"], [5])
+        seq = [(bank(5, 384 * c, WID[c]), T.idn[:], B("yr", c)[:, qj(c, a, j)], a + j == 0, a + j == 6) for j in range(4)]
+        mm(seq, ["idn", "yr%d%d" % (c, a)], ["dsum%d" % c], [5])
 
     def spk_nd(t, c):
         sm, w = T["sM%d%d" % (t, c)], WID[c]
-        SC(lambda s: s.activation(sm[:, w:2 * w], bank(5, 0, w), F.Relu, bias=1.0, scale=-float(2.0 ** 80)), ["dsum"], ["nd%d%d" % (t, c)], [5])
-        send(t, T["rM%d%d" % (t, c)][:], sm[:], "msg%d%d" % (t, c), ["sx%d%d" % (t, c), "nd%d%d" % (t, c)], ["rm%d%d" % (t, c)])
+        V(lambda v: v.tensor_scalar(B("nv", c)[:], bank(5, 384 * c, w), 0.0, 1024.0, A.is_le, A.mult), ["dsum%d" % c], ["nv%d" % c], [5])
+        V(lambda v: v.tensor_tensor(sm[:], B("nv", c)[:], (bank(0, 0, 4 * w, 4), bank(1, 0, w) if OPT["sq"] else bank(1, 0, 4 * w, 4))[c], A.add), ["nv%d" % c, "x0d%d" % c], ["sm%d%d" % (t, c)], [c])
+        send(t, T["rM%d%d" % (t, c)][:], sm[:], "msg%d%d" % (t, c), ["sm%d%d" % (t, c)], ["rm%d%d" % (t, c)])
 
-    def mask1(c):
+    def mask_f(c, a):
         w = WID[c]
-        seq = [(bank(5, 128, w), ek(a + 4 * j), B("z", c)[:, qj(c, a, j)], a + j == 0, a + j == 6) for a in range(4) for j in range(4)]
-        mm(seq, ekk + ["z%d%d" % (c, a) for a in range(4)], ["F"], [5])
-        SC(lambda s: s.activation(B("fk", c)[:], bank(5, 128, w), F.Copy), ["F"], ["fk%d" % c], [5])
+        seq = [(bank(2, 0, w), ek(a + 4 * j), B("z", c)[:, qj(c, a, j)], a + j == 0, a + j == 6) for j in range(4)]
+        mm(seq, ekk + ["z%d%d" % (c, a)], ["wd0"], [2])
 
-    def mask2(c):
+    def mask_k(c):
         w = WID[c]
-        mm([(bank(5, 256, w), T.m2[:], B("fk", c)[:], True, True)], ["m2", "fk%d" % c], ["mp"], [5])
-        V(lambda v: v.tensor_scalar(B("mk", c)[:], bank(5, 256, w), T.tc[:], None, A.is_gt), ["mp", "tc"], ["mk%d" % c], [5])
+        SC(lambda s: s.activation(B("fk", c)[:], bank(2, 0, w), F.Copy), ["wd0"], ["fk%d" % c], [2])
+        mm([(bank(5, 256 + 192 * c, w), T.m2[:], B("fk", c)[:], True, True)], ["m2", "fk%d" % c], ["mp%d" % c], [5])
+
+    def mask_m(c):
+        w = WID[c]
+        V(lambda v: v.tensor_scalar(B("mk", c)[:], bank(5, 256 + 192 * c, w), T.tc[:], None, A.is_gt), ["mp%d" % c, "tc"], ["mk%d" % c], [5])
 
     def mask3(c):
         SC(lambda s: s.activation(B("km", c)[:], B("mk", c)[:], F.Copy, bias=1.0, scale=-1.0), ["mk%d" % c], ["km%d" % c])
@@ -322,32 +341,44 @@ def rank_program(g, core, T, topo):
 
     def hear_in(t, c):
         rm, w = T["rM%d%d" % (t, c)], WID[c]
-        seq = []
-        for j in range(4):
-            seq.append((bank(xb(c), j, 4 * w, 4), T.idn[:], rm[:, 0:w], True, False))
-            seq.append((bank(xb(c), j, 4 * w, 4), T.ibig[:], rm[:, w:2 * w], False, True))
-        mm(seq, ["idn", "ibig", "rm%d%d" % (t, c)], ["xm%d" % c], [xb(c)])
+        mm([(bank(xb(c), j, 4 * w - j, 4), T.i16[:], rm[:], True, True) for j in range(4)], ["i16", "rm%d%d" % (t, c)], ["xm%d" % c], [xb(c)])
 
-    def hear_pre(t, c):
+    def hear_nd(t, c):
+        V(lambda v: v.tensor_scalar(B("nd", c)[:], T["rM%d%d" % (t, c)][:], 512.0, None, A.is_ge), ["rm%d%d" % (t, c)], ["nd%d" % c])
+
+    def hear_px(t, c):
         rm, w = T["rM%d%d" % (t, c)], WID[c]
-        mm([(bank(c, 0, w), T.idn[:], rm[:, 0:w], True, True),
-            (bank(c, w, w), T.idn[:], B("rW", t)[:, sl(c)], True, True)],
-           ["idn", "rm%d%d" % (t, c), "rw%d" % t], ["pre%d" % c], [c])
+        mm([(bank(c, 0, w), T.i16[:], rm[:], True, False), (bank(c, 0, w), T.ibig[:], B("nd", c)[:], False, True)],
+           ["i16", "ibig", "nd%d" % c, "rm%d%d" % (t, c)], ["pre%d" % c], [c])
         if t < RO - 1:
-            SC(lambda s: s.activation(B("de", c)[:], rm[:, w:2 * w], F.Copy, bias=1.0, scale=-1.0), ["rm%d%d" % (t, c)], ["de%d" % c])
+            SC(lambda s: s.activation(B("de", c)[:], B("nd", c)[:], F.Copy, bias=1.0, scale=-1.0), ["nd%d" % c], ["de%d" % c])
+
+    def hear_pw(t, c):
+        w = WID[c]
+        mm([(bank(c, w, w), T.idn[:], B("rW", t)[:, sl(c)], True, True)], ["idn", "rw%d" % t], ["pw%d" % c], [c])
+
+    def hear_nx(t, c):
+        w = WID[c]
+        if t < RO - 1:
             V(lambda v: v.tensor_tensor(B("nx", c)[:], B("de", c)[:], bank(c, 0, w), A.mult), ["de%d" % c, "pre%d" % c], ["nx%d" % c], [c])
 
     def hear_cmp(c, a):
-        V(lambda v: v.tensor_tensor(B("e", c)[:, qr(c, a)], B("yg", c)[:, a:16 * WID[c]:4], bank(xb(c), 0, 4 * WID[c]), A.not_equal),
-          gk("yg", c) + ["xm%d" % c], ["e%d%d" % (c, a)], [xb(c)])
+        V(lambda v: v.tensor_tensor(B("yr", c)[:, qr(c, a)], B("yg", c)[:, a:16 * WID[c]:4], bank(xb(c), 0, 4 * WID[c]), A.not_equal),
+          gk("yg", c) + ["xm%d" % c], ["yr%d%d" % (c, a)], [xb(c)])
 
     def hear_cnt(t, c, a):
         seq, w = [], WID[c]
-        if a == 0:
-            seq.append((bank(hb(c), 0, w), T.nb[:], T["rM%d%d" % (t, c)][:, w:2 * w], True, False))
+        if a == 1:
+            seq.append((bank(hb(c), 0, w), T.nb[:], B("nd", c)[:], False, False))
         for j in range(4):
-            seq.append((bank(hb(c), 0, w), ek(a + 4 * j), B("e", c)[:, qj(c, a, j)], False, a + j == 6))
-        mm(seq, ekk + ["nb", "rm%d%d" % (t, c), "e%d%d" % (c, a)], ["miss%d" % c], [hb(c)])
+            seq.append((bank(hb(c), 0, w), ek(a + 4 * j), B("yr", c)[:, qj(c, a, j)], a + j == 0, a + j == 6))
+        mm(seq, ekk + ["yr%d%d" % (c, a)] + (["nb", "nd%d" % c] if a else []), ["miss%d" % c], [hb(c)])
+
+    def hear_b(t, a):
+        hear_cmp(1, a)
+        if a == 0:
+            hear_nd(t, 1)
+        hear_cnt(t, 1, a)
 
     def pick1(t, c):
         h, w = hb(c), WID[c]
@@ -389,20 +420,21 @@ def rank_program(g, core, T, topo):
 
     def post_na(t, c):
         lt, n, w = T["L%d%d" % (t, c)], WID[c] // 16, WID[c]
-        V(lambda v: v.tensor_tensor(B("na", c)[:], T.xs[:, :].indirect(lt[:, 0:n]), T["rM%d%d" % (t, c)][:, w:2 * w], A.mult),
-          ["xs", "L%d" % c, "rm%d%d" % (t, c)], ["na%d" % c])
+        V(lambda v: v.tensor_tensor(B("na", c)[:], T.xs[:, :].indirect(lt[:, 0:n]), B("nd", c)[:], A.mult),
+          ["xs", "L%d" % c, "nd%d" % c], ["na%d" % c])
 
     def post_un(t, c):
         w = WID[c]
         V(lambda v: v.tensor_tensor(B("un", c)[:], B("ys", c)[:], bank(c, 0, w), A.not_equal), ["ys%d" % c, "pre%d" % c], ["un%d" % c], [c])
-        V(lambda v: v.tensor_tensor(B("zf", c)[:], B("un", c)[:], bank(c, w, w), A.mult), ["un%d" % c, "pre%d" % c], ["zf%d" % c], [c])
-        mm([(bank(4, 0, w), T.bo[:], B("un", c)[:], True, True), (bank(4, 128, w), T.m1[:], B("zf", c)[:], True, True)],
-           ["bo", "m1", "un%d" % c, "zf%d" % c], ["UY"], [4])
+        V(lambda v: v.tensor_tensor(B("zf", c)[:], B("un", c)[:], bank(c, w, w), A.mult), ["un%d" % c, "pw%d" % c], ["zf%d" % c], [c])
+        u = 4 - c
+        mm([(bank(u, 0, w), T.bo[:], B("un", c)[:], True, True), (bank(u, 128, w), T.m1[:], B("zf", c)[:], True, True)],
+           ["bo", "m1", "un%d" % c, "zf%d" % c], ["UY%d" % c], [u])
 
     def post_phi(t, c):
-        w = WID[c]
-        V(lambda v: v.tensor_tensor(B("tt", c)[:], bank(4, 0, w), B("rW", t)[:, S + LO[c]:S + LO[c] + w], A.is_le), ["UY", "rw%d" % t], ["tt%d" % c], [4])
-        V(lambda v: v.tensor_tensor(B("sP", t)[:, sl(c)], bank(4, 128, w), B("tt", c)[:], A.is_gt), ["UY", "tt%d" % c], ["sp%d%d" % (t, c)], [4])
+        w, u = WID[c], 4 - c
+        V(lambda v: v.tensor_tensor(B("tt", c)[:], bank(u, 0, w), B("rW", t)[:, S + LO[c]:S + LO[c] + w], A.is_le), ["UY%d" % c, "rw%d" % t], ["tt%d" % c], [u])
+        V(lambda v: v.tensor_tensor(B("sP", t)[:, sl(c)], bank(u, 128, w), B("tt", c)[:], A.is_gt), ["UY%d" % c, "tt%d" % c], ["sp%d%d" % (t, c)], [u])
 
     def send_phi(t):
         send(t, B("rP", t)[:], B("sP", t)[:], "phi%d" % t, ["sp%d%d" % (t, c) for c in range(NC)], ["rp%d" % t])
@@ -430,17 +462,17 @@ def rank_program(g, core, T, topo):
 
     def rup1(t):
         move1(B("rP", t), ["rp%d" % t], T.rb, "rb", T.p1)
-        mm([(bank(5, 0, S), T.bo[:], B("rP", t)[:], True, True)], ["bo", "rp%d" % t], ["Fo"], [5])
+        mm([(bank(5, 320, S), T.bo[:], B("rP", t)[:], True, True)], ["bo", "rp%d" % t], ["Fo"], [5])
 
     def rup2(t):
         move2(T.rb, "rb", T.t1)
 
     def rup3(t):
         V(lambda v: v.tensor_copy(T.rb2[:], bank(4, 0, S)), ["RR"], ["rb2"], [4])
-        move1(B("sP", t), ["sp%d%d" % (t, c) for c in range(NC)], T.rb2, "rb2", T.p2)
+        move1(B("sP", t), ["sp%d%d" % (t, c) for c in range(NC)], T.rb2, "rb2", T.p1)
 
     def rup4(t):
-        move2(T.rb2, "rb2", T.t2)
+        move2(T.rb2, "rb2", T.t1)
         if t < RO - 1:
             SC(lambda s: s.activation(B("sW", t + 1)[:, 0:S], bank(4, 0, S), F.Exp, scale=-5.0 * math.log(2.0)), ["RR"], ["w%d" % (t + 1)], [4])
         else:
@@ -448,15 +480,18 @@ def rank_program(g, core, T, topo):
             dma("Y", T.ypref[:], T.rout[:], "o2", ["rout"], [])
 
     def rup5(t):
-        V(lambda v: v.tensor_copy(T.rb[:], bank(4, 0, S)), ["RR"], ["rb"], [4])
+        SC(lambda s: s.activation(T.rb[:], bank(4, 0, S), F.Copy), ["RR"], ["rb"], [4])
 
     def aup(t):
         if t < RO - 1:
-            V(lambda v: v.tensor_tensor(T.a32[:], bank(5, 0, S), T.a32[:], A.add), ["Fo"], ["a32"], [5])
+            V(lambda v: v.tensor_tensor(T.a32[:], bank(5, 320, S), T.a32[:], A.add), ["Fo"], ["a32"], [5])
         else:
-            V(lambda v: v.tensor_tensor(T.aout[:], bank(5, 0, S), T.a32[:], A.add), ["Fo", "a32"], ["aout"], [5])
+            V(lambda v: v.tensor_tensor(T.aout[:], bank(5, 320, S), T.a32[:], A.add), ["Fo", "a32"], ["aout"], [5])
             dma("S", T.yfail[:], T.aout[0:128:16, :], "o3", ["aout"], [])
 
+    cb = OPT["cb"]
+    if OPT["sq"]:
+        cb = 0
     for t in range(RO):
         if t == 0:
             gx("S", 0, 0)
@@ -467,110 +502,131 @@ def rank_program(g, core, T, topo):
             wdup(t, 0)
             for a in range(4):
                 spk_cmp(0, a)
-            counts()
-            x0dup(1)
+            if OPT["sq"]:
+                for a in range(4):
+                    dif_b(a)
+                x0one()
+            else:
+                x0dup(1)
             wdup(t, 1)
+            counts()
             thr(t)
         else:
             x0dup(0)
-            for a in range(4):
-                spk_cmp(0, a)
-                if a == 0:
-                    cupd(t - 1, 1)
-                    gx("S", 1, 0)
+            cupd(t - 1, 1)
+            gx("S", 1, 0)
+            spk_cmp(0, 0)
             rup1(t - 1)
-            gy("S", 0, 0)
-            x0copy(t, 0)
+            spk_cmp(0, 1)
             rup2(t - 1)
-            x0dup(1)
-            spk_cmp(1, 0)
+            spk_cmp(0, 2)
             rup3(t - 1)
-            spk_cmp(1, 1)
+            if OPT["sq"]:
+                dif_b(0)
+            else:
+                x0dup(1)
+            spk_cmp(0, 3)
             rup4(t - 1)
-            wdup(t, 0)
-            spk_cmp(1, 2)
-            spk_cmp(1, 3)
-            wdup(t, 1)
-            rup5(t - 1)
+            for a in range(cb):
+                spk_cmp(1, a)
             aup(t - 1)
             thr(t)
-        if t == 0:
-            x0copy(t, 0)
+            if OPT["sq"]:
+                dif_b(1)
+            wdup(t, 0)
+            if OPT["sq"]:
+                dif_b(2)
+                dif_b(3)
+                x0one()
+            rup5(t - 1)
+            wdup(t, 1)
         for a in range(4):
             spk_wt(0, a)
             spk_y(0, a)
+            if a == OPT["sqa"] and OPT["sq"]:
+                sqr_b()
             spk_relu(0, a)
             if a > 0:
                 spk_sum(0, a - 1)
-        x0copy(t, 1)
-        if t == 0:
-            spk_cmp(1, 0)
-        spk_wt(1, 0)
-        spk_sum(0, 3)
-        spk_nd(t, 0)
         for a in range(4):
-            if a:
-                if t == 0:
-                    spk_cmp(1, a)
-                spk_wt(1, a)
+            if not OPT["sq"] and (t == 0 or a >= cb):
+                spk_cmp(1, a)
+            spk_wt(1, a)
             spk_y(1, a)
-            spk_relu(1, a)
-            if a:
+            if a < OPT["vr"]:
+                spk_relu(1, a)
+            if a == 0:
+                spk_sum(0, 3)
+            elif a <= OPT["vr"]:
                 spk_sum(1, a - 1)
-        spk_sum(1, 3)
+            if OPT["mf"]:
+                mask_f(0, a)
+            if a == OPT["nda"]:
+                spk_nd(t, 0)
+        for a in range(OPT["vr"], 4):
+            spk_relu(1, a)
+            spk_sum(1, a)
+        if OPT["vr"] == 4:
+            spk_sum(1, 3)
         spk_nd(t, 1)
+        if not OPT["mf"]:
+            for a in range(4):
+                mask_f(0, a)
         if t == 0:
             late_constants()
-            gy("V", 0, 0)
-            gy("S", 0, 1)
-        else:
-            gy("V", 1, 0)
-            gy("S", 0, 1)
-        mask1(0)
-        mask2(0)
-        mask1(1)
-        mask2(1)
-        if t == 0:
-            gy("S", 1, 0)
+        gy("V", 0, 0)
+        mask_k(0)
+        gy("S", 0, 1)
+        for a in range(4):
+            mask_f(1, a)
+        mask_k(1)
+        gy("S", 1, 0)
         hear_in(t, 0)
         for a in range(4):
             hear_cmp(0, a)
+            if a == 0:
+                hear_nd(t, 0)
             hear_cnt(t, 0, a)
+            if a == 1:
+                hear_in(t, 1)
         pick1(t, 0)
-        mask3(0)
-        mask3(1)
-        hear_pre(t, 0)
+        hear_b(t, 0)
+        hear_b(t, 1)
         pick2(t, 0)
-        hear_in(t, 1)
-        hear_cmp(1, 0)
-        hear_cnt(t, 1, 0)
-        hear_cmp(1, 1)
-        hear_cnt(t, 1, 1)
+        mask_m(0)
+        hear_b(t, 2)
+        hear_b(t, 3)
+        pick1(t, 1)
+        hear_px(t, 0)
         pick3(t, 0)
         post_y(t, 0)
-        for a in (2, 3):
-            hear_cmp(1, a)
-            hear_cnt(t, 1, a)
-        pick1(t, 1)
-        hear_pre(t, 1)
-        post_h(t, 0)
+        hear_nx(t, 0)
+        if t < RO - 1:
+            post_na(t, 0)
         pick2(t, 1)
+        hear_px(t, 1)
+        hear_pw(t, 0)
+        hear_pw(t, 1)
+        mask_m(1)
+        mask3(0)
         post_un(t, 0)
+        hear_nx(t, 1)
+        mask3(1)
+        post_h(t, 0)
         pick3(t, 1)
         post_y(t, 1)
         if t < RO - 1:
-            post_na(t, 0)
             post_na(t, 1)
-            scatter(t, 0)
-            scatter(t, 1)
         post_phi(t, 0)
         post_un(t, 1)
         if t < RO - 1:
-            post_h(t, 1)
+            scatter(t, 0)
         post_phi(t, 1)
         send_phi(t)
+        if t < RO - 1:
+            scatter(t, 1)
+        post_h(t, 1)
         if t == RO - 1:
-            post_h(t, 1)
             dma("Y", T.ycand[:], T.hf[:], "o1", ["hf0", "hf1"], [])
         cupd(t, 0)
         if t < RO - 1:

@@ -17,12 +17,12 @@ SCRATCH = {
     "fi": ("sbuf", [8, S], "int32"), "fb": ("sbuf", [8, S], "bfloat16"),
     "cf": ("sbuf", [128, S], "float32"), "cu": ("sbuf", [128, S], "uint16"),
     "hf": ("sbuf", [128, S], "float32"), "hu": ("sbuf", [128, S], "uint16"), "hm16": ("sbuf", [128, S], "float16"),
-    "rb": ("sbuf", [128, S], "bfloat16"), "rb2": ("sbuf", [128, S], "bfloat16"), "rout": ("sbuf", [128, S], "float32"),
-    "a32": ("sbuf", [128, S], "int32"), "a3": ("sbuf", [128, S], "int32"), "aout": ("sbuf", [128, S], "float32"),
+    "rb": ("sbuf", [128, S], "bfloat16"), "rb2": ("sbuf", [128, S], "bfloat16"), "rout": ("sbuf", [128, 2 * S], "float32"),
+    "a32": ("sbuf", [128, S], "int32"), "a3": ("sbuf", [128, S], "int32"),
     "p1": ("sbuf", [128, S], "bfloat16"), "t1": ("sbuf", [128, S], "bfloat16"),
     "ones": ("sbuf", [128, 128], "bfloat16"), "idn": ("sbuf", [128, 128], "bfloat16"), "bo0": ("sbuf", [128, 128], "bfloat16"),
     "bo": ("sbuf", [128, 128], "bfloat16"), "k8a": ("sbuf", [8, 128], "bfloat16"), "k8": ("sbuf", [8, 128], "bfloat16"),
-    "mtmp": ("sbuf", [128, 384], "bfloat16"), "m1": ("sbuf", [128, 128], "bfloat16"), "m2": ("sbuf", [128, 128], "bfloat16"),
+    "mtmp": ("sbuf", [128, 896], "bfloat16"), "lw": ("sbuf", [128, 1], "float32"), "m1": ("sbuf", [128, 128], "bfloat16"), "m2": ("sbuf", [128, 128], "bfloat16"),
     "m3": ("sbuf", [128, 128], "bfloat16"), "nb": ("sbuf", [128, 128], "bfloat16"), "ni": ("sbuf", [128, 128], "bfloat16"),
     "ibig": ("sbuf", [128, 128], "bfloat16"), "i16": ("sbuf", [128, 128], "float16"),
     "ek": ("sbuf", [128, 2048], "bfloat16"), "ek16": ("sbuf", [128, 2048], "float16"),
@@ -53,9 +53,10 @@ for _t in range(RO):
     SCRATCH["rW%d" % _t] = ("sbuf", [128, 2 * S], "bfloat16")
     SEMAPHORES += ["wth%d" % _t, "phi%d" % _t]
 
-OPT = {"sq": 0, "sqa": 0, "nda": 3, "mf": 0, "vr": 2, "cb": 2}
+OPT = {"sq": 0, "nda": 3, "vr": 2, "cb": 0}
 QS = {"V": "sv", "S": "ss", "P": "sp", "G": "sg"}
 LNB = 0.96 * math.log(2.0)
+LNW = 5.0 * math.log(2.0)
 
 
 def tracker(g, T):
@@ -188,6 +189,9 @@ def rank_program(g, core, T, topo):
     SC(lambda s: s.activation(T.nb[:], T.bo[:], F.Copy, scale=-1.0), ["bo"], ["nb"])
     SC(lambda s: s.activation(T.ni[:], T.idn[:], F.Copy, scale=-1.0), ["idn"], ["ni"])
     SC(lambda s: s.activation(T.ibig[:], T.idn[:], F.Copy, scale=-1024.0), ["idn"], ["ibig"])
+    for i in range(4):
+        SC(lambda s: s.activation(T.mtmp[:, 384 + 128 * i:512 + 128 * i], T.idn[:], F.Copy, scale=float(2.0 ** (5 * i - 20))), ["idn"], ["iw"] if i == 3 else ["iw%d" % i])
+    V(lambda v: v.memset(T.lw[:], -5.0 * LNW), (), ["lw"])
     V(lambda v: v.memset(T.ek[:], 0.0), (), ["ek"])
     for k in range(16):
         V(lambda v: v.tensor_copy(T.ek[:, 129 * k:129 * k + 113:16], T.bo[:, 0:128:16]), ["bo", "ek"], ["ek_%d" % k])
@@ -199,7 +203,7 @@ def rank_program(g, core, T, topo):
 
     def orders():
         V(lambda v: v.tensor_copy(T.rb[:], T.ri[:]), ["ri"], ["rb"])
-        SC(lambda s: s.activation(T.sW0[:, 0:S], T.rb[:], F.Exp, scale=-5.0 * math.log(2.0)), ["rb"], ["w0"])
+        SC(lambda s: s.activation(T.sW0[:, 0:S], T.rb[:], F.Exp, bias=T.lw[:], scale=-LNW), ["rb", "lw"], ["w00", "w01"])
 
     def counts():
         V(lambda v: v.tensor_copy(T.fb[:], T.fi[:]), ["fi"], ["fb"])
@@ -222,6 +226,9 @@ def rank_program(g, core, T, topo):
         V(lambda v: v.tensor_copy(T.cf[:], T.ci[:]), ["ci"], ["cf0", "cf1"])
         V(lambda v: v.tensor_copy(T.hf[:], T.hi[:]), ["hi"], ["hf0", "hf1"])
         V(lambda v: v.tensor_scalar(T.hm16[:], T.hi[:], -2048.0, None, A.add), ["hi"], ["hm160", "hm161"])
+
+    def iw(i):
+        return T.mtmp[:, 384 + 128 * i:512 + 128 * i]
 
     def ek(k):
         return T.ek[:, 128 * k:128 * k + 128]
@@ -256,7 +263,7 @@ def rank_program(g, core, T, topo):
         sw = B("sW", t)
         V(lambda v: v.tensor_scalar(T.a3[:], T.a32[:], 3, None, A.bitwise_and), ["a32"], ["a3"])
         V(lambda v: v.tensor_scalar(sw[:, S:2 * S], T.a3[:], 5.5, None, A.add), ["a3"], ["thr%d" % t])
-        send(t, B("rW", t)[:], sw[:], "wth%d" % t, ["w%d" % t, "thr%d" % t], ["rw%d" % t])
+        send(t, B("rW", t)[:], sw[:], "wth%d" % t, ["w%d0" % t, "w%d1" % t, "thr%d" % t], ["rw%d" % t])
 
     def x0dup(c):
         mm([(bank(c, j, 4 * WID[c], 4), T.idn[:], B("xg", c)[:, 0:16 * WID[c]:16], True, True) for j in range(4)],
@@ -267,8 +274,20 @@ def rank_program(g, core, T, topo):
 
     def wdup(t, c):
         b, o = wdb(c)
-        mm([(bank(b, o + j, 4 * WID[c] - j, 4), T.idn[:], B("sW", t)[:, sl(c)], True, True) for j in range(4)],
-           ["idn", "w%d" % t], ["wd%d" % c], [b])
+        if t == 0:
+            mm([(bank(b, o + j, 4 * WID[c] - j, 4), T.idn[:], T.sW0[:, sl(c)], True, True) for j in range(4)], ["idn", "w00", "w01"], ["wd%d" % c], [b])
+            return
+        seq = []
+        for j in range(4):
+            out = bank(b, o + j, 4 * WID[c] - j, 4)
+            seq += [(out, T.idn[:], B("sW", t - 1)[:, sl(c)], True, False),
+                    (out, iw(2 * t - 1), B("sP", t - 1)[:, sl(c)], False, False),
+                    (out, iw(2 * t - 2), B("rP", t - 1)[:, sl(c)], False, True)]
+        mm(seq, ["idn", "iw", "w%d%d" % (t - 1, c), "sp%d%d" % (t - 1, c), "rp%d" % (t - 1)], ["wd%d" % c], [b])
+
+    def wcopy(t, c):
+        b, o = wdb(c)
+        SC(lambda s: s.activation(B("sW", t)[:, sl(c)], bank(b, o, 4 * WID[c], 4), F.Copy), ["wd%d" % c], ["w%d%d" % (t, c)], [b])
 
     def spk_cmp(c, a):
         V(lambda v: v.tensor_tensor(B("z", c)[:, qr(c, a)], B("xg", c)[:, a:16 * WID[c]:4], bank(c, 0, 4 * WID[c]), A.not_equal),
@@ -317,12 +336,12 @@ def rank_program(g, core, T, topo):
 
     def mask_f(c, a):
         w = WID[c]
-        seq = [(bank(2, 0, w), ek(a + 4 * j), B("z", c)[:, qj(c, a, j)], a + j == 0, a + j == 6) for j in range(4)]
-        mm(seq, ekk + ["z%d%d" % (c, a)], ["wd0"], [2])
+        seq = [(bank(5, 128 - 128 * c, w), ek(a + 4 * j), B("z", c)[:, qj(c, a, j)], a + j == 0, a + j == 6) for j in range(4)]
+        mm(seq, ekk + ["z%d%d" % (c, a)], ["F%d" % c] + ["dsum0"][:c], [5])
 
     def mask_k(c):
         w = WID[c]
-        SC(lambda s: s.activation(B("fk", c)[:], bank(2, 0, w), F.Copy), ["wd0"], ["fk%d" % c], [2])
+        SC(lambda s: s.activation(B("fk", c)[:], bank(5, 128 - 128 * c, w), F.Copy), ["F%d" % c], ["fk%d" % c], [5])
         mm([(bank(5, 256 + 192 * c, w), T.m2[:], B("fk", c)[:], True, True)], ["m2", "fk%d" % c], ["mp%d" % c], [5])
 
     def mask_m(c):
@@ -451,43 +470,42 @@ def rank_program(g, core, T, topo):
         if t < RO - 1:
             V(lambda v: v.tensor_copy(T.cu[:, sl(c)], T.cf[:, sl(c)]), ["cf%d" % c], ["cu%d" % c])
 
-    def move1(phi, pk, rb, rk, pb):
+    def move1(phi, pk, rb, rk, pb, m):
         V(lambda v: v.tensor_tensor(pb[:], phi[:], rb[:], A.mult), [rk] + pk, [pb.name])
-        mm([(bank(3, 0, S), T.bo[:], pb[:], True, True)], ["bo", pb.name], ["rf"], [3])
-        mm([(bank(4, 0, S), T.idn[:], rb[:], True, False), (bank(4, 0, S), T.ni[:], pb[:], False, False)], ["idn", "ni", rk, pb.name], ["RR"], [4])
+        mm([(bank(m, 0, S), T.bo[:], pb[:], True, True)], ["bo", pb.name], ["rf"], [m])
+        mm([(bank(m + 1, 0, S), T.idn[:], rb[:], True, False), (bank(m + 1, 0, S), T.ni[:], pb[:], False, False)],
+           ["idn", "ni", rk, pb.name], ["RR"], [m + 1])
 
-    def move2(rb, rk, tb):
-        V(lambda v: v.tensor_tensor(tb[:], bank(3, 0, S), rb[:], A.is_gt), ["rf", rk], [tb.name], [3])
-        mm([(bank(4, 0, S), T.idn[:], tb[:], False, True)], ["idn", tb.name], ["RR"], [4])
+    def move2(rb, rk, tb, m):
+        V(lambda v: v.tensor_tensor(tb[:], bank(m, 0, S), rb[:], A.is_gt), ["rf", rk], [tb.name], [m])
+        mm([(bank(m + 1, 0, S), T.idn[:], tb[:], False, True)], ["idn", tb.name], ["RR"], [m + 1])
 
     def rup1(t):
-        move1(B("rP", t), ["rp%d" % t], T.rb, "rb", T.p1)
-        mm([(bank(5, 320, S), T.bo[:], B("rP", t)[:], True, True)], ["bo", "rp%d" % t], ["Fo"], [5])
+        move1(B("rP", t), ["rp%d" % t], T.rb, "rb", T.p1, 0)
+        mm([(bank(0, 192, S), T.bo[:], B("rP", t)[:], True, True)], ["bo", "rp%d" % t], ["Fo"], [0])
 
     def rup2(t):
-        move2(T.rb, "rb", T.t1)
+        move2(T.rb, "rb", T.t1, 0)
 
     def rup3(t):
-        V(lambda v: v.tensor_copy(T.rb2[:], bank(4, 0, S)), ["RR"], ["rb2"], [4])
-        move1(B("sP", t), ["sp%d%d" % (t, c) for c in range(NC)], T.rb2, "rb2", T.p1)
+        V(lambda v: v.tensor_copy(T.rb2[:], bank(1, 0, S)), ["RR"], ["rb2"], [1])
+        move1(B("sP", t), ["sp%d%d" % (t, c) for c in range(NC)], T.rb2, "rb2", T.p1, 2)
 
     def rup4(t):
-        move2(T.rb2, "rb2", T.t1)
-        if t < RO - 1:
-            SC(lambda s: s.activation(B("sW", t + 1)[:, 0:S], bank(4, 0, S), F.Exp, scale=-5.0 * math.log(2.0)), ["RR"], ["w%d" % (t + 1)], [4])
-        else:
-            V(lambda v: v.tensor_copy(T.rout[:], bank(4, 0, S)), ["RR"], ["rout"], [4])
-            dma("Y", T.ypref[:], T.rout[:], "o2", ["rout"], [])
+        move2(T.rb2, "rb2", T.t1, 2)
+        if t == RO - 1:
+            V(lambda v: v.tensor_copy(T.rout[:, 0:S], bank(3, 0, S)), ["RR"], ["rout"], [3])
+            dma("Y", T.ypref[:], T.rout[:, 0:S], "o2", ["rout"], [])
 
     def rup5(t):
-        SC(lambda s: s.activation(T.rb[:], bank(4, 0, S), F.Copy), ["RR"], ["rb"], [4])
+        SC(lambda s: s.activation(T.rb[:], bank(3, 0, S), F.Copy), ["RR"], ["rb"], [3])
 
     def aup(t):
         if t < RO - 1:
-            V(lambda v: v.tensor_tensor(T.a32[:], bank(5, 320, S), T.a32[:], A.add), ["Fo"], ["a32"], [5])
+            V(lambda v: v.tensor_tensor(T.a32[:], bank(0, 192, S), T.a32[:], A.add), ["Fo"], ["a32"], [0])
         else:
-            V(lambda v: v.tensor_tensor(T.aout[:], bank(5, 320, S), T.a32[:], A.add), ["Fo", "a32"], ["aout"], [5])
-            dma("S", T.yfail[:], T.aout[0:128:16, :], "o3", ["aout"], [])
+            V(lambda v: v.tensor_tensor(T.rout[:, S:2 * S], bank(0, 192, S), T.a32[:], A.add), ["Fo", "a32"], ["aout"], [0])
+            dma("S", T.yfail[:], T.rout[0:128:16, S:2 * S], "o3", ["aout"], [])
 
     cb = OPT["cb"]
     if OPT["sq"]:
@@ -502,12 +520,7 @@ def rank_program(g, core, T, topo):
             wdup(t, 0)
             for a in range(4):
                 spk_cmp(0, a)
-            if OPT["sq"]:
-                for a in range(4):
-                    dif_b(a)
-                x0one()
-            else:
-                x0dup(1)
+            x0dup(1)
             wdup(t, 1)
             counts()
             thr(t)
@@ -515,41 +528,22 @@ def rank_program(g, core, T, topo):
             x0dup(0)
             cupd(t - 1, 1)
             gx("S", 1, 0)
-            spk_cmp(0, 0)
-            rup1(t - 1)
-            spk_cmp(0, 1)
-            rup2(t - 1)
-            spk_cmp(0, 2)
-            rup3(t - 1)
-            if OPT["sq"]:
-                dif_b(0)
-            else:
-                x0dup(1)
-            spk_cmp(0, 3)
-            rup4(t - 1)
+            for a in range(4):
+                spk_cmp(0, a)
+            wdup(t, 0)
+            wcopy(t, 0)
+            x0dup(1)
+            wdup(t, 1)
             for a in range(cb):
                 spk_cmp(1, a)
-            aup(t - 1)
-            thr(t)
-            if OPT["sq"]:
-                dif_b(1)
-            wdup(t, 0)
-            if OPT["sq"]:
-                dif_b(2)
-                dif_b(3)
-                x0one()
-            rup5(t - 1)
-            wdup(t, 1)
         for a in range(4):
             spk_wt(0, a)
             spk_y(0, a)
-            if a == OPT["sqa"] and OPT["sq"]:
-                sqr_b()
             spk_relu(0, a)
             if a > 0:
                 spk_sum(0, a - 1)
         for a in range(4):
-            if not OPT["sq"] and (t == 0 or a >= cb):
+            if t == 0 or a >= cb:
                 spk_cmp(1, a)
             spk_wt(1, a)
             spk_y(1, a)
@@ -559,8 +553,6 @@ def rank_program(g, core, T, topo):
                 spk_sum(0, 3)
             elif a <= OPT["vr"]:
                 spk_sum(1, a - 1)
-            if OPT["mf"]:
-                mask_f(0, a)
             if a == OPT["nda"]:
                 spk_nd(t, 0)
         for a in range(OPT["vr"], 4):
@@ -569,17 +561,21 @@ def rank_program(g, core, T, topo):
         if OPT["vr"] == 4:
             spk_sum(1, 3)
         spk_nd(t, 1)
-        if not OPT["mf"]:
-            for a in range(4):
-                mask_f(0, a)
         if t == 0:
             late_constants()
+        else:
+            wcopy(t, 1)
+            rup1(t - 1)
+        for a in range(4):
+            mask_f(0, a)
         gy("V", 0, 0)
-        mask_k(0)
         gy("S", 0, 1)
+        if t > 0:
+            rup2(t - 1)
+            aup(t - 1)
+            thr(t)
         for a in range(4):
             mask_f(1, a)
-        mask_k(1)
         gy("S", 1, 0)
         hear_in(t, 0)
         for a in range(4):
@@ -589,6 +585,7 @@ def rank_program(g, core, T, topo):
             hear_cnt(t, 0, a)
             if a == 1:
                 hear_in(t, 1)
+        mask_k(0)
         pick1(t, 0)
         hear_b(t, 0)
         hear_b(t, 1)
@@ -597,41 +594,48 @@ def rank_program(g, core, T, topo):
         hear_b(t, 2)
         hear_b(t, 3)
         pick1(t, 1)
+        if t > 0:
+            rup3(t - 1)
+        mask_k(1)
         hear_px(t, 0)
         pick3(t, 0)
         post_y(t, 0)
         hear_nx(t, 0)
         if t < RO - 1:
             post_na(t, 0)
+        mask3(0)
         pick2(t, 1)
+        if t > 0:
+            rup4(t - 1)
+        post_h(t, 0)
         hear_px(t, 1)
         hear_pw(t, 0)
         hear_pw(t, 1)
-        mask_m(1)
-        mask3(0)
-        post_un(t, 0)
-        hear_nx(t, 1)
-        mask3(1)
-        post_h(t, 0)
         pick3(t, 1)
         post_y(t, 1)
+        if t > 0:
+            rup5(t - 1)
         if t < RO - 1:
             post_na(t, 1)
-        post_phi(t, 0)
+        post_un(t, 0)
         post_un(t, 1)
+        post_phi(t, 0)
+        hear_nx(t, 1)
         if t < RO - 1:
             scatter(t, 0)
         post_phi(t, 1)
         send_phi(t)
         if t < RO - 1:
             scatter(t, 1)
-        post_h(t, 1)
-        if t == RO - 1:
-            dma("Y", T.ycand[:], T.hf[:], "o1", ["hf0", "hf1"], [])
+        mask_m(1)
         cupd(t, 0)
+        mask3(1)
         if t < RO - 1:
             gx("V", 0, 0)
             gx("S", 0, 1)
+        post_h(t, 1)
+        if t == RO - 1:
+            dma("Y", T.ycand[:], T.hf[:], "o1", ["hf0", "hf1"], [])
     cupd(RO - 1, 1)
     dma("Y", T.yctx[:], T.cf[:], "o0", ["cf0", "cf1"], [])
     rup1(RO - 1)

@@ -325,12 +325,12 @@ def rank_program(g, core, T, topo):
         SC(lambda s: s.activation(B("yr", c)[:, qr(c, a)], bank(bb, 0, 4 * WID[c]), F.Relu), ["Y%d" % bb], ["yr%d%d" % (c, a)], [bb])
 
     def spk_sum(c, a):
-        seq = [(bank(5, 384 * c, WID[c]), T.idn[:], B("yr", c)[:, qj(c, a, j)], a + j == 0, a + j == 6) for j in range(4)]
-        mm(seq, ["idn", "yr%d%d" % (c, a)], ["dsum%d" % c], [5])
+        seq = [(bank(5 + c, 384 * c, WID[c]), T.idn[:], B("yr", c)[:, qj(c, a, j)], a + j == 0, a + j == 6) for j in range(4)]
+        mm(seq, ["idn", "yr%d%d" % (c, a)], ["dsum%d" % c], [5 + c])
 
     def spk_nd(t, c):
         sm, w = T["sM%d%d" % (t, c)], WID[c]
-        V(lambda v: v.tensor_scalar(B("nv", c)[:], bank(5, 384 * c, w), 0.0, 1024.0, A.is_le, A.mult), ["dsum%d" % c], ["nv%d" % c], [5])
+        V(lambda v: v.tensor_scalar(B("nv", c)[:], bank(5 + c, 384 * c, w), 0.0, 1024.0, A.is_le, A.mult), ["dsum%d" % c], ["nv%d" % c], [5 + c])
         V(lambda v: v.tensor_tensor(sm[:], B("nv", c)[:], (bank(0, 0, 4 * w, 4), bank(1, 0, w) if OPT["sq"] else bank(1, 0, 4 * w, 4))[c], A.add), ["nv%d" % c, "x0d%d" % c], ["sm%d%d" % (t, c)], [c])
         send(t, T["rM%d%d" % (t, c)][:], sm[:], "msg%d%d" % (t, c), ["sm%d%d" % (t, c)], ["rm%d%d" % (t, c)])
 
@@ -493,19 +493,40 @@ def rank_program(g, core, T, topo):
 
     def rup4(t):
         move2(T.rb2, "rb2", T.t1, 2)
-        if t == RO - 1:
-            V(lambda v: v.tensor_copy(T.rout[:, 0:S], bank(3, 0, S)), ["RR"], ["rout"], [3])
-            dma("Y", T.ypref[:], T.rout[:, 0:S], "o2", ["rout"], [])
+
+    def last_orders1():
+        sp = B("sP", RO - 1)
+        sk = ["sp%d%d" % (RO - 1, c) for c in range(NC)]
+        V(lambda v: v.tensor_tensor(T.p1[:], sp[:], T.rb[:], A.mult), ["rb"] + sk, ["p1"])
+        mm([(bank(2, 0, S), T.bo[:], T.p1[:], True, True)], ["bo", "p1"], ["rf"], [2])
+        V(lambda v: v.tensor_tensor(T.t1[:], bank(2, 0, S), T.rb[:], A.is_gt), ["rf", "rb"], ["t1"], [2])
+        m = [(T.idn[:], T.rb[:]), (T.ni[:], T.p1[:]), (T.idn[:], T.t1[:])]
+        seq = []
+        for out, terms in ((bank(7, 0, S), m + [(T.mtmp[:, 128:256], sp[:])]), (bank(6, 0, S), m),
+                           (bank(6, 192, S), m + [(T.nb[:], sp[:]), (T.idn[:], sp[:])])):
+            seq += [(out, l, r, i == 0, i == len(terms) - 1) for i, (l, r) in enumerate(terms)]
+        mm(seq, ["idn", "ni", "nb", "mt1", "rb", "p1", "t1"] + sk, ["MK"], [6, 7])
+        SC(lambda s: s.activation(T.rb2[:], bank(7, 0, S), F.Copy), ["MK"], ["rb2"], [7])
+
+    def last_orders2():
+        rp = B("rP", RO - 1)
+        rk = ["rp%d" % (RO - 1)]
+        V(lambda v: v.tensor_tensor(T.p1[:], rp[:], bank(6, 0, S), A.mult), ["MK"] + rk, ["p1"], [6])
+        mm([(bank(5, 0, S), T.bo[:], T.p1[:], True, True)], ["bo", "p1"], ["m1f"], [5])
+        V(lambda v: v.tensor_tensor(T.t1[:], rp[:], bank(6, 192, S), A.mult), ["MK"] + rk, ["t1"], [6])
+        V(lambda v: v.tensor_tensor(bank(0, 0, S), bank(6, 0, S), T.t1[:], A.subtract), ["MK", "t1"], ["dd"], [6, 0])
+        V(lambda v: v.tensor_tensor(T.p1[:], bank(5, 0, S), T.rb2[:], A.is_gt), ["m1f", "rb2"], ["p1"], [5])
+        V(lambda v: v.tensor_tensor(T.rout[:, 0:S], T.p1[:], bank(0, 0, S), A.add), ["p1", "dd"], ["rout"], [0])
+        dma("Y", T.ypref[:], T.rout[:, 0:S], "o2", ["rout"], [])
+        mm([(bank(4, 192, S), T.bo[:], rp[:], True, True)], ["bo"] + rk, ["Fo"], [4])
+        V(lambda v: v.tensor_tensor(T.rout[:, S:2 * S], bank(4, 192, S), T.a32[:], A.add), ["Fo", "a32"], ["aout"], [4])
+        dma("S", T.yfail[:], T.rout[0:128:16, S:2 * S], "o3", ["aout"], [])
 
     def rup5(t):
         SC(lambda s: s.activation(T.rb[:], bank(3, 0, S), F.Copy), ["RR"], ["rb"], [3])
 
     def aup(t):
-        if t < RO - 1:
-            V(lambda v: v.tensor_tensor(T.a32[:], bank(0, 192, S), T.a32[:], A.add), ["Fo"], ["a32"], [0])
-        else:
-            V(lambda v: v.tensor_tensor(T.rout[:, S:2 * S], bank(0, 192, S), T.a32[:], A.add), ["Fo", "a32"], ["aout"], [0])
-            dma("S", T.yfail[:], T.rout[0:128:16, S:2 * S], "o3", ["aout"], [])
+        V(lambda v: v.tensor_tensor(T.a32[:], bank(0, 192, S), T.a32[:], A.add), ["Fo"], ["a32"], [0])
 
     cb = OPT["cb"]
     if OPT["sq"]:
@@ -574,6 +595,7 @@ def rank_program(g, core, T, topo):
             rup2(t - 1)
             aup(t - 1)
             thr(t)
+            post_h(t - 1, 1)
         for a in range(4):
             mask_f(1, a)
         gy("S", 1, 0)
@@ -620,12 +642,11 @@ def rank_program(g, core, T, topo):
         post_un(t, 0)
         post_un(t, 1)
         post_phi(t, 0)
+        post_phi(t, 1)
+        send_phi(t)
         hear_nx(t, 1)
         if t < RO - 1:
             scatter(t, 0)
-        post_phi(t, 1)
-        send_phi(t)
-        if t < RO - 1:
             scatter(t, 1)
         mask_m(1)
         cupd(t, 0)
@@ -633,16 +654,13 @@ def rank_program(g, core, T, topo):
         if t < RO - 1:
             gx("V", 0, 0)
             gx("S", 0, 1)
-        post_h(t, 1)
-        if t == RO - 1:
+        else:
+            post_h(t, 1)
             dma("Y", T.ycand[:], T.hf[:], "o1", ["hf0", "hf1"], [])
+            last_orders1()
     cupd(RO - 1, 1)
     dma("Y", T.yctx[:], T.cf[:], "o0", ["cf0", "cf1"], [])
-    rup1(RO - 1)
-    rup2(RO - 1)
-    rup3(RO - 1)
-    rup4(RO - 1)
-    aup(RO - 1)
+    last_orders2()
     for s in ("o0", "o1", "o2", "o3"):
         g.sync.wait_ge(T.sem[s], 16)
     for q in ("V", "S", "P", "G"):

import math
import numpy as np
from concourse.mybir import AluOpType as A, ActivationFunctionType as F

RO = 3
S = 192
WID = [128, 64]
LO = [0, 128]
NC = 2
H0 = 64

SCRATCH = {
    "ps": ("psum", [128, 4096], "float32"),
    "xs": ("sbuf", [128, 4096], "bfloat16"),
    "az": ("sbuf", [128, 4096], "int32"),
    "ci": ("sbuf", [128, S], "int32"), "hi": ("sbuf", [128, S], "int32"), "ri": ("sbuf", [128, S], "int32"),
    "fi": ("sbuf", [8, S], "int32"), "fb": ("sbuf", [8, S], "bfloat16"),
    "cf": ("sbuf", [128, S], "float32"), "cu": ("sbuf", [128, S], "uint16"),
    "hf": ("sbuf", [128, S], "float32"), "hu": ("sbuf", [128, S], "uint16"), "hm16": ("sbuf", [128, S], "float16"),
    "rb": ("sbuf", [128, S], "bfloat16"), "rb2": ("sbuf", [128, S], "bfloat16"), "rout": ("sbuf", [128, 2 * S], "float32"),
    "a32": ("sbuf", [128, S], "int32"), "a3": ("sbuf", [128, S], "int32"),
    "p1": ("sbuf", [128, S], "bfloat16"), "t1": ("sbuf", [128, S], "bfloat16"),
    "ones": ("sbuf", [128, 128], "bfloat16"), "idn": ("sbuf", [128, 128], "bfloat16"), "bo0": ("sbuf", [128, 128], "bfloat16"),
    "bo": ("sbuf", [128, 128], "bfloat16"), "k8a": ("sbuf", [8, 128], "bfloat16"), "k8": ("sbuf", [8, 128], "bfloat16"),
    "mtmp": ("sbuf", [128, 896], "bfloat16"), "lw": ("sbuf", [128, 1], "float32"), "m1": ("sbuf", [128, 128], "bfloat16"), "m2": ("sbuf", [128, 128], "bfloat16"),
    "m3": ("sbuf", [128, 128], "bfloat16"), "nb": ("sbuf", [128, 128], "bfloat16"), "ni": ("sbuf", [128, 128], "bfloat16"),
    "ibig": ("sbuf", [128, 128], "bfloat16"), "i16": ("sbuf", [128, 128], "float16"),
    "ek": ("sbuf", [128, 2048], "bfloat16"), "ek16": ("sbuf", [128, 2048], "float16"),
    "pi": ("sbuf", [128, 1], "int32"), "ki": ("sbuf", [128, 1], "int32"), "kc": ("sbuf", [128, 1], "float32"),
    "k16": ("sbuf", [128, 1], "float32"), "bk": ("sbuf", [128, 1], "float32"), "tc": ("sbuf", [128, 1], "float32"),
    "rowq": ("sbuf", [128, 12], "float32"),
}
SEMAPHORES = ["sv", "ss", "sp", "sg", "lctx", "lcand", "lpref", "lfail", "lx", "las", "loc", "o0", "o1", "o2", "o3"]
for _c in range(NC):
    _w = WID[_c]
    for _n, _k, _d in (("xg", 16, "bfloat16"), ("yg", 16, "bfloat16"), ("z", 16, "bfloat16"), ("yr", 16, "bfloat16"), ("nv", 1, "float32"), ("nd", 1, "bfloat16"),
                       ("fk", 1, "bfloat16"), ("mk", 1, "float32"), ("km", 1, "float32"), ("ck", 1, "float32"), ("ct", 1, "float32"),
                       ("wk", 1, "bfloat16"), ("ow", 1, "float16"), ("pr", 2, "float16"), ("hm", 1, "float32"), ("hd", 1, "float32"),
                       ("ys", 1, "bfloat16"), ("un", 1, "bfloat16"), ("zf", 1, "bfloat16"), ("tt", 1, "float32"), ("de", 1, "bfloat16"),
                       ("na", 1, "bfloat16"), ("nx", 1, "bfloat16")):
        SCRATCH["%s%d" % (_n, _c)] = ("sbuf", [128, _k * _w], _d)
    SCRATCH["cs%d" % _c] = ("sbuf", [128, _w // 8], "float16")
    for _t in range(RO):
        SCRATCH["sM%d%d" % (_t, _c)] = ("sbuf", [128, _w], "float16")
        SCRATCH["rM%d%d" % (_t, _c)] = ("sbuf", [128, _w], "float16")
        SCRATCH["L%d%d" % (_t, _c)] = ("sbuf", [128, _w // 8], "uint16")
        SCRATCH["rL%d%d" % (_t, _c)] = ("sbuf", [128, _w // 16], "uint16")
        SEMAPHORES += ["msg%d%d" % (_t, _c), "lst%d%d" % (_t, _c)]
for _t in range(RO):
    SCRATCH["sP%d" % _t] = ("sbuf", [128, S], "bfloat16")
    SCRATCH["rP%d" % _t] = ("sbuf", [128, S], "bfloat16")
    SCRATCH["sW%d" % _t] = ("sbuf", [128, 2 * S], "bfloat16")
    SCRATCH["rW%d" % _t] = ("sbuf", [128, 2 * S], "bfloat16")
    SEMAPHORES += ["wth%d" % _t, "phi%d" % _t]

OPT = {"sq": 0, "nda": 3, "vr": 2, "cb": 0}
QS = {"V": "sv", "S": "ss", "P": "sp", "G": "sg"}
LNB = 0.96 * math.log(2.0)
LNW = 5.0 * math.log(2.0)


def tracker(g, T):
    qq = {"V": g.vector, "S": g.scalar, "P": g.tensor, "G": g, "Y": g.sync}
    seen = {q: {} for q in qq}
    know = {}
    cnt = {q: 0 for q in QS}
    lastw, readers, bank = {}, {}, {}

    def need(q, tok):
        s, n = tok
        if seen[q].get(s, 0) >= n:
            return
        qq[q].wait_ge(T.sem[s], n)
        for k, v in list(know.get(tok, {}).items()) + [(s, n)]:
            if seen[q].get(k, 0) < v:
                seen[q][k] = v

    def before(q, r, w, b):
        toks = {}
        for k in r:
            if k in lastw:
                s, n = lastw[k]
                toks[s] = max(toks.get(s, 0), n)
        for k in w:
            for s, n in ([lastw[k]] if k in lastw else []) + readers.get(k, []):
                toks[s] = max(toks.get(s, 0), n)
        for k in b:
            for q2, (s, n) in bank.get(k, {}).items():
                if q2 != q:
                    toks[s] = max(toks.get(s, 0), n)
        own = QS.get(q)
        for s in sorted(toks, key=lambda s: s == own):
            need(q, (s, toks[s]))

    def after(q, tok, r, w, b):
        know[tok] = dict(seen[q])
        for k in r:
            readers.setdefault(k, []).append(tok)
        for k in w:
            lastw[k] = tok
            readers[k] = []
        for k in b:
            bank.setdefault(k, {})[q] = tok

    def op(q, call, r=(), w=(), b=()):
        before(q, r, w, b)
        ins = call(qq[q])
        cnt[q] += 1
        ins.then_inc(T.sem[QS[q]], 1)
        after(q, (QS[q], cnt[q]), r, w, b)

    def mm(seq, r, w, b):
        before("P", r, w, b)
        ins = None
        for out, lhsT, rhs, start, stop in seq:
            ins = g.tensor.matmul(out, lhsT, rhs, start, stop)
        cnt["P"] += 1
        ins.then_inc(T.sem["sp"], 1)
        after("P", ("sp", cnt["P"]), r, w, b)

    def dma(q, out, in_, sem, r=(), w=()):
        before(q, r, w, ())
        qq[q].dma_start(out, in_).then_inc(T.sem[sem], 16)
        after(q, (sem, 16), r, w, ())

    def mark(key, tok):
        lastw[key] = tok

    return {"op": op, "mm": mm, "dma": dma, "before": before, "need": need, "mark": mark, "cnt": cnt}


def rank_program(g, core, T, topo):
    rank = T.rank_of(core)
    if rank is None:
        return
    K = tracker(g, T)
    op, mm, dma = K["op"], K["mm"], K["dma"]
    nloc = [0]

    def V(call, r=(), w=(), b=()):
        op("V", call, r, w, b)

    def SC(call, r=(), w=(), b=()):
        op("S", call, r, w, b)

    def bank(i, lo, n, step=1):
        return T.ps[:, 512 * i + lo:512 * i + lo + n:step]

    def B(name, c):
        return T["%s%d" % (name, c)]

    def send(t, out, in_, sem, rk, wk):
        peer = T.cores[rank ^ (1 << t)]
        rid, pid = topo.addr(peer)[:2]
        ne = len(topo.engines(core, peer))
        K["before"]("G", rk, (), ())
        g.remote_dma(out_ap=out, in_ap=in_, remote_sem=T.sem[sem], local_sem=T.sem["loc"], pid=pid, routing_id=rid,
                     dma_engine_mask=topo.mask(core, peer))
        nloc[0] += ne
        for k in wk:
            K["mark"](k, (sem, ne))

    def sl(c):
        return slice(LO[c], LO[c] + WID[c])

    def qr(c, a):
        return slice(4 * WID[c] * a, 4 * WID[c] * (a + 1))

    def qj(c, a, j):
        return slice(4 * WID[c] * a + j, 4 * WID[c] * (a + 1), 4)

    dma("S", T.ci[:], T.ctx[:], "lctx", (), ["ci"])
    dma("Y", T.xs[:], T.x[:], "lx", (), ["xs"])
    dma("S", T.ri[:], T.pref[:], "lpref", (), ["ri"])
    dma("S", T.hi[:], T.cand[:], "lcand", (), ["hi"])
    dma("S", T.fi[:], T.fail0[:], "lfail", (), ["fi"])
    dma("Y", T.az[:], T.assoc[:], "las", ["xs"], ["az"])
    V(lambda v: v.memset(T.ones[:], 1.0), (), ["ones"])
    op("G", lambda e: e.affine_select(T.bo0[:], T.ones[:], [[-16, 8], [0, 16]], A.is_ge, 0.0, 0, 1), ["ones"], ["bo0"])
    op("G", lambda e: e.affine_select(T.bo[:], T.bo0[:], [[16, 8], [0, 16]], A.is_ge, 0.0, 15, -1), ["bo0"], ["bo"])
    op("G", lambda e: e.affine_select(T.idn[:], T.ones[:], [[-1, 128]], A.is_equal, 0.0, 0, 1), ["ones"], ["idn"])
    op("G", lambda e: e.affine_select(T.k8a[:], T.ones[0:8, :], [[1, 128]], A.is_ge, 0.0, 0, -16), ["ones"], ["k8a"])
    op("G", lambda e: e.affine_select(T.k8[:], T.k8a[:], [[-1, 128]], A.is_ge, 0.0, 15, 16), ["k8a"], ["k8"])
    op("G", lambda e: e.iota(T.pi[:], [[1, 1]], 0, 1), (), ["pi"])
    op("G", lambda e: e.iota(T.rowq[:], [[256, 12]], 0, 0, allow_small_or_imprecise_dtypes=True), (), ["rowq"])
    SC(lambda s: s.activation(T.mtmp[:, 0:128], T.idn[:], F.Copy, scale=2.0), ["idn"], ["mt0"])
    SC(lambda s: s.activation(T.mtmp[:, 128:256], T.idn[:], F.Copy, scale=16.0), ["idn"], ["mt1"])
    SC(lambda s: s.activation(T.mtmp[:, 256:384], T.bo[:], F.Copy, scale=0.41), ["bo"], ["mt2"])
    SC(lambda s: s.activation(T.nb[:], T.bo[:], F.Copy, scale=-1.0), ["bo"], ["nb"])
    SC(lambda s: s.activation(T.ni[:], T.idn[:], F.Copy, scale=-1.0), ["idn"], ["ni"])
    SC(lambda s: s.activation(T.ibig[:], T.idn[:], F.Copy, scale=-1024.0), ["idn"], ["ibig"])
    for i in range(4):
        SC(lambda s: s.activation(T.mtmp[:, 384 + 128 * i:512 + 128 * i], T.idn[:], F.Copy, scale=float(2.0 ** (5 * i - 20))), ["idn"], ["iw"] if i == 3 else ["iw%d" % i])
    V(lambda v: v.memset(T.lw[:], -5.0 * LNW), (), ["lw"])
    V(lambda v: v.memset(T.ek[:], 0.0), (), ["ek"])
    for k in range(16):
        V(lambda v: v.tensor_copy(T.ek[:, 129 * k:129 * k + 113:16], T.bo[:, 0:128:16]), ["bo", "ek"], ["ek_%d" % k])
    ekk = ["ek_%d" % k for k in range(16)]
    V(lambda v: v.tensor_tensor(T.m1[:], T.mtmp[:, 0:128], T.bo[:], A.subtract), ["mt0", "bo"], ["m1"])
    V(lambda v: v.tensor_scalar(T.ki[:], T.pi[:], 15, None, A.bitwise_and), ["pi"], ["ki"])
    V(lambda v: v.tensor_copy(T.kc[:], T.ki[:]), ["ki"], ["kc"])
    V(lambda v: v.tensor_copy(T.cu[:], T.ci[:]), ["ci"], ["cu0", "cu1"])

    def orders():
        V(lambda v: v.tensor_copy(T.rb[:], T.ri[:]), ["ri"], ["rb"])
        SC(lambda s: s.activation(T.sW0[:, 0:S], T.rb[:], F.Exp, bias=T.lw[:], scale=-LNW), ["rb", "lw"], ["w00", "w01"])

    def counts():
        V(lambda v: v.tensor_copy(T.fb[:], T.fi[:]), ["fi"], ["fb"])
        mm([(bank(5, 320, S), T.k8[:], T.fb[:], True, True)], ["k8", "fb"], ["A0"], [5])
        V(lambda v: v.tensor_copy(T.hu[:], T.hi[:]), ["hi"], ["hu0", "hu1"])
        V(lambda v: v.tensor_copy(T.a32[:], bank(5, 320, S)), ["A0"], ["a32"], [5])

    def late_constants():
        V(lambda v: v.tensor_tensor(T.m2[:], T.mtmp[:, 128:256], T.bo[:], A.subtract), ["mt1", "bo"], ["m2"])
        V(lambda v: v.tensor_tensor(T.m3[:], T.idn[:], T.mtmp[:, 256:384], A.subtract), ["mt2", "idn"], ["m3"])
        V(lambda v: v.tensor_copy(T.i16[:], T.idn[:]), ["idn"], ["i16"])
        V(lambda v: v.tensor_copy(T.ek16[:], T.ek[:]), ekk, ["ek16"])
        V(lambda v: v.tensor_scalar(T.k16[:], T.kc[:], 16.0, None, A.mult), ["kc"], ["k16"])
        V(lambda v: v.tensor_scalar(T.bk[:], T.kc[:], -LNB, 84.5, A.mult, A.add), ["kc"], ["bk"])
        V(lambda v: v.tensor_scalar(T.tc[:], T.kc[:], 0.0, -1e29, A.is_equal, A.mult), ["kc"], ["tc"])
        for c in range(NC):
            n, o = WID[c] // 16, LO[c] // 16
            V(lambda v: v.tensor_scalar(B("cs", c)[:, 0:n], T.rowq[:, 0:n], 0.0, 2048.0, A.mult, A.add), ["rowq"], ["csa%d" % c])
            V(lambda v: v.tensor_scalar(B("cs", c)[:, n:2 * n], T.rowq[:, o:o + n], T.k16[:], None, A.add), ["rowq", "k16"], ["csb%d" % c])
        V(lambda v: v.tensor_copy(T.cf[:], T.ci[:]), ["ci"], ["cf0", "cf1"])
        V(lambda v: v.tensor_copy(T.hf[:], T.hi[:]), ["hi"], ["hf0", "hf1"])
        V(lambda v: v.tensor_scalar(T.hm16[:], T.hi[:], -2048.0, None, A.add), ["hi"], ["hm160", "hm161"])

    def iw(i):
        return T.mtmp[:, 384 + 128 * i:512 + 128 * i]

    def ek(k):
        return T.ek[:, 128 * k:128 * k + 128]

    def ek16(k):
        return T.ek16[:, 128 * k:128 * k + 128]

    def pieces(c):
        return list(range(WID[c] // H0))

    def gather(q, which, c, p):
        name, lst = (("xg", T.cu), ("yg", T.hu))[which]
        lkey = ("cu%d", "hu%d")[which] % c
        dst = B(name, c)[:, 16 * H0 * p:16 * H0 * (p + 1)]
        src = T.xs[:, :].indirect(lst[:, LO[c] + H0 * p:LO[c] + H0 * (p + 1)])
        key = "%s%d_%d" % (name, c, p)
        if q == "V":
            V(lambda v: v.tensor_copy(dst, src), [lkey, "xs"], [key])
        else:
            SC(lambda s: s.activation(dst, src, F.Copy), [lkey, "xs"], [key])

    def gx(q, c, p):
        gather(q, 0, c, p)

    def gy(q, c, p):
        gather(q, 1, c, p)

    def gk(name, c):
        return ["%s%d_%d" % (name, c, p) for p in pieces(c)]

    def thr(t):
        sw = B("sW", t)
        V(lambda v: v.tensor_scalar(T.a3[:], T.a32[:], 3, None, A.bitwise_and), ["a32"], ["a3"])
        V(lambda v: v.tensor_scalar(sw[:, S:2 * S], T.a3[:], 5.5, None, A.add), ["a3"], ["thr%d" % t])
        send(t, B("rW", t)[:], sw[:], "wth%d" % t, ["w%d0" % t, "w%d1" % t, "thr%d" % t], ["rw%d" % t])

    def x0dup(c):
        mm([(bank(c, j, 4 * WID[c], 4), T.idn[:], B("xg", c)[:, 0:16 * WID[c]:16], True, True) for j in range(4)],
           ["idn"] + gk("xg", c), ["x0d%d" % c], [c])

    def wdb(c):
        return ((2, 0), (1, 256))[c]

    def wdup(t, c):
        b, o = wdb(c)
        if t == 0:
            mm([(bank(b, o + j, 4 * WID[c] - j, 4), T.idn[:], T.sW0[:, sl(c)], True, True) for j in range(4)], ["idn", "w00", "w01"], ["wd%d" % c], [b])
            return
        seq = []
        for j in range(4):
            out = bank(b, o + j, 4 * WID[c] - j, 4)
            seq += [(out, T.idn[:], B("sW", t - 1)[:, sl(c)], True, False),
                    (out, iw(2 * t - 1), B("sP", t - 1)[:, sl(c)], False, False),
                    (out, iw(2 * t - 2), B("rP", t - 1)[:, sl(c)], False, True)]
        mm(seq, ["idn", "iw", "w%d%d" % (t - 1, c), "sp%d%d" % (t - 1, c), "rp%d" % (t - 1)], ["wd%d" % c], [b])

    def wcopy(t, c):
        b, o = wdb(c)
        SC(lambda s: s.activation(B("sW", t)[:, sl(c)], bank(b, o, 4 * WID[c], 4), F.Copy), ["wd%d" % c], ["w%d%d" % (t, c)], [b])

    def spk_cmp(c, a):
        V(lambda v: v.tensor_tensor(B("z", c)[:, qr(c, a)], B("xg", c)[:, a:16 * WID[c]:4], bank(c, 0, 4 * WID[c]), A.not_equal),
          gk("xg", c) + ["x0d%d" % c], ["z%d%d" % (c, a)], [c])

    def dif_b(a):
        w, c = WID[1], 1
        o = 4 * w * a
        seq = [(bank(6, o, 4 * w), T.idn[:], B("xg", c)[:, a:16 * w:4], True, False)]
        seq += [(bank(6, o + j, 4 * w - j, 4), T.ni[:], B("xg", c)[:, 0:16 * w:16], False, j == 3) for j in range(4)]
        mm(seq, ["idn", "ni"] + gk("xg", c), ["dif%d" % a], [6 + a // 2])

    def sqr_b():
        w = WID[1]
        SC(lambda s: s.activation(T.z1[:, 0:16 * w], bank(6, 0, 16 * w), F.Square), ["dif%d" % a for a in range(4)], ["z1%d" % a for a in range(4)], [6, 7])

    def x0one():
        w = WID[1]
        mm([(bank(1, 0, w), T.idn[:], T.xg1[:, 0:16 * w:16], True, True)], ["idn"] + gk("xg", 1), ["x0d1"], [1])

    def spk_wt(c, a):
        z = B("z", c)[:, qr(c, a)]
        b, o = wdb(c)
        V(lambda v: v.tensor_tensor(z, z, bank(b, o, 4 * WID[c]), A.min), ["wd%d" % c], ["z%d%d" % (c, a)], [b])

    def spk_y(c, a):
        bb = 3 + a % 2
        mm([(bank(bb, 0, 4 * WID[c]), T.m1[:], B("z", c)[:, qr(c, a)], True, True)], ["m1", "z%d%d" % (c, a)], ["Y%d" % bb], [bb])

    def spk_relu(c, a):
        bb = 3 + a % 2
        if c == 1 and a >= OPT["vr"]:
            V(lambda v: v.tensor_scalar(B("yr", c)[:, qr(c, a)], bank(bb, 0, 4 * WID[c]), 0.0, None, A.max), ["Y%d" % bb], ["yr%d%d" % (c, a)], [bb])
            return
        SC(lambda s: s.activation(B("yr", c)[:, qr(c, a)], bank(bb, 0, 4 * WID[c]), F.Relu), ["Y%d" % bb], ["yr%d%d" % (c, a)], [bb])

    def spk_sum(c, a):
        seq = [(bank(5 + c, 384 * c, WID[c]), T.idn[:], B("yr", c)[:, qj(c, a, j)], a + j == 0, a + j == 6) for j in range(4)]
        mm(seq, ["idn", "yr%d%d" % (c, a)], ["dsum%d" % c], [5 + c])

    def spk_nd(t, c):
        sm, w = T["sM%d%d" % (t, c)], WID[c]
        V(lambda v: v.tensor_scalar(B("nv", c)[:], bank(5 + c, 384 * c, w), 0.0, 1024.0, A.is_le, A.mult), ["dsum%d" % c], ["nv%d" % c], [5 + c])
        V(lambda v: v.tensor_tensor(sm[:], B("nv", c)[:], (bank(0, 0, 4 * w, 4), bank(1, 0, w) if OPT["sq"] else bank(1, 0, 4 * w, 4))[c], A.add), ["nv%d" % c, "x0d%d" % c], ["sm%d%d" % (t, c)], [c])
        send(t, T["rM%d%d" % (t, c)][:], sm[:], "msg%d%d" % (t, c), ["sm%d%d" % (t, c)], ["rm%d%d" % (t, c)])

    def mask_f(c, a):
        w = WID[c]
        seq = [(bank(5, 128 - 128 * c, w), ek(a + 4 * j), B("z", c)[:, qj(c, a, j)], a + j == 0, a + j == 6) for j in range(4)]
        mm(seq, ekk + ["z%d%d" % (c, a)], ["F%d" % c] + ["dsum0"][:c], [5])

    def mask_k(c):
        w = WID[c]
        SC(lambda s: s.activation(B("fk", c)[:], bank(5, 128 - 128 * c, w), F.Copy), ["F%d" % c], ["fk%d" % c], [5])
        mm([(bank(5, 256 + 192 * c, w), T.m2[:], B("fk", c)[:], True, True)], ["m2", "fk%d" % c], ["mp%d" % c], [5])

    def mask_m(c):
        w = WID[c]
        V(lambda v: v.tensor_scalar(B("mk", c)[:], bank(5, 256 + 192 * c, w), T.tc[:], None, A.is_gt), ["mp%d" % c, "tc"], ["mk%d" % c], [5])

    def mask3(c):
        SC(lambda s: s.activation(B("km", c)[:], B("mk", c)[:], F.Copy, bias=1.0, scale=-1.0), ["mk%d" % c], ["km%d" % c])
        V(lambda v: v.tensor_tensor(B("ck", c)[:], T.cf[:, sl(c)], B("km", c)[:], A.mult), ["cf%d" % c, "km%d" % c], ["ck%d" % c])

    def xb(c):
        return 2 + c

    def hb(c):
        return 7 - c

    def hear_in(t, c):
        rm, w = T["rM%d%d" % (t, c)], WID[c]
        mm([(bank(xb(c), j, 4 * w - j, 4), T.i16[:], rm[:], True, True) for j in range(4)], ["i16", "rm%d%d" % (t, c)], ["xm%d" % c], [xb(c)])

    def hear_nd(t, c):
        V(lambda v: v.tensor_scalar(B("nd", c)[:], T["rM%d%d" % (t, c)][:], 512.0, None, A.is_ge), ["rm%d%d" % (t, c)], ["nd%d" % c])

    def hear_px(t, c):
        rm, w = T["rM%d%d" % (t, c)], WID[c]
        mm([(bank(c, 0, w), T.i16[:], rm[:], True, False), (bank(c, 0, w), T.ibig[:], B("nd", c)[:], False, True)],
           ["i16", "ibig", "nd%d" % c, "rm%d%d" % (t, c)], ["pre%d" % c], [c])
        if t < RO - 1:
            SC(lambda s: s.activation(B("de", c)[:], B("nd", c)[:], F.Copy, bias=1.0, scale=-1.0), ["nd%d" % c], ["de%d" % c])

    def hear_pw(t, c):
        w = WID[c]
        mm([(bank(c, w, w), T.idn[:], B("rW", t)[:, sl(c)], True, True)], ["idn", "rw%d" % t], ["pw%d" % c], [c])

    def hear_nx(t, c):
        w = WID[c]
        if t < RO - 1:
            V(lambda v: v.tensor_tensor(B("nx", c)[:], B("de", c)[:], bank(c, 0, w), A.mult), ["de%d" % c, "pre%d" % c], ["nx%d" % c], [c])

    def hear_cmp(c, a):
        V(lambda v: v.tensor_tensor(B("yr", c)[:, qr(c, a)], B("yg", c)[:, a:16 * WID[c]:4], bank(xb(c), 0, 4 * WID[c]), A.not_equal),
          gk("yg", c) + ["xm%d" % c], ["yr%d%d" % (c, a)], [xb(c)])

    def hear_cnt(t, c, a):
        seq, w = [], WID[c]
        if a == 1:
            seq.append((bank(hb(c), 0, w), T.nb[:], B("nd", c)[:], False, False))
        for j in range(4):
            seq.append((bank(hb(c), 0, w), ek(a + 4 * j), B("yr", c)[:, qj(c, a, j)], a + j == 0, a + j == 6))
        mm(seq, ekk + ["yr%d%d" % (c, a)] + (["nb", "nd%d" % c] if a else []), ["miss%d" % c], [hb(c)])

    def hear_b(t, a):
        hear_cmp(1, a)
        if a == 0:
            hear_nd(t, 1)
        hear_cnt(t, 1, a)

    def pick1(t, c):
        h, w = hb(c), WID[c]
        SC(lambda s: s.activation(B("wk", c)[:], bank(h, 0, w), F.Exp, bias=T.bk[:], scale=-16.0 * LNB), ["miss%d" % c, "bk"], ["wk%d" % c], [h])
        SC(lambda s: s.activation(B("hm", c)[:], bank(h, 0, w), F.Sign), ["miss%d" % c], ["hm%d" % c], [h])
        mm([(bank(h, 128, w), T.m3[:], B("wk", c)[:], True, True)], ["m3", "wk%d" % c], ["G%d" % c], [h])

    def pick2(t, c):
        h, w = hb(c), WID[c]
        pr, n = B("pr", c), WID[c] // 8
        V(lambda v: v.tensor_scalar(B("ow", c)[:], bank(h, 128, w), 0.0, None, A.is_gt), ["G%d" % c], ["ow%d" % c], [h])
        V(lambda v: v.tensor_scalar(pr[:, w:2 * w], bank(h, 128, w), 0.0, T.kc[:], A.is_gt, A.mult), ["G%d" % c, "kc"], ["prq%d" % c], [h])
        V(lambda v: v.tensor_tensor(pr[:, 0:w], B("ow", c)[:], T.hm16[:, sl(c)], A.mult), ["ow%d" % c, "hm16%d" % c], ["prn%d" % c])
        seq = [(bank(h, 256, n), T.i16[:], B("cs", c)[:], True, False)]
        for k in range(16):
            seq.append((bank(h, 256, n), ek16(k), pr[:, k:2 * w:16], False, k == 15))
        mm(seq, ["i16", "csa%d" % c, "csb%d" % c, "ek16", "prq%d" % c, "prn%d" % c], ["lp%d" % c], [h])

    def pick3(t, c):
        h, n = hb(c), WID[c] // 16
        lt = T["L%d%d" % (t, c)]
        V(lambda v: v.tensor_copy(lt[:], bank(h, 256, 2 * n)), ["lp%d" % c], ["L%d" % c], [h])
        send(t, T["rL%d%d" % (t, c)][:], lt[:, 0:n], "lst%d%d" % (t, c), ["L%d" % c], ["rl%d%d" % (t, c)])

    def post_h(t, c):
        hf, n = T.hf[:, sl(c)], WID[c] // 16
        lt = T["L%d%d" % (t, c)]
        hd = B("hd", c)
        V(lambda v: v.tensor_tensor(hd[:], T.az[:, :].indirect(lt[:, 0:n]), hf, A.subtract), ["az", "L%d" % c, "hf%d" % c], ["hd%d" % c])
        V(lambda v: v.tensor_tensor(hd[:], hd[:], B("hm", c)[:], A.mult), ["hm%d" % c], ["hd%d" % c])
        V(lambda v: v.tensor_tensor(hf, hf, hd[:], A.add), ["hd%d" % c], ["hf%d" % c])
        if t < RO - 1:
            V(lambda v: v.tensor_copy(T.hu[:, sl(c)], hf), ["hf%d" % c], ["hu%d" % c])
            V(lambda v: v.tensor_scalar(T.hm16[:, sl(c)], hf, -2048.0, None, A.add), ["hf%d" % c], ["hm16%d" % c])

    def post_y(t, c):
        lt, n = T["L%d%d" % (t, c)], WID[c] // 16
        SC(lambda s: s.activation(B("ys", c)[:], T.xs[:, :].indirect(lt[:, 0:n]), F.Copy), ["xs", "L%d" % c], ["ys%d" % c])

    def post_na(t, c):
        lt, n, w = T["L%d%d" % (t, c)], WID[c] // 16, WID[c]
        V(lambda v: v.tensor_tensor(B("na", c)[:], T.xs[:, :].indirect(lt[:, 0:n]), B("nd", c)[:], A.mult),
          ["xs", "L%d" % c, "nd%d" % c], ["na%d" % c])

    def post_un(t, c):
        w = WID[c]
        V(lambda v: v.tensor_tensor(B("un", c)[:], B("ys", c)[:], bank(c, 0, w), A.not_equal), ["ys%d" % c, "pre%d" % c], ["un%d" % c], [c])
        V(lambda v: v.tensor_tensor(B("zf", c)[:], B("un", c)[:], bank(c, w, w), A.mult), ["un%d" % c, "pw%d" % c], ["zf%d" % c], [c])
        u = 4 - c
        mm([(bank(u, 0, w), T.bo[:], B("un", c)[:], True, True), (bank(u, 128, w), T.m1[:], B("zf", c)[:], True, True)],
           ["bo", "m1", "un%d" % c, "zf%d" % c], ["UY%d" % c], [u])

    def post_phi(t, c):
        w, u = WID[c], 4 - c
        V(lambda v: v.tensor_tensor(B("tt", c)[:], bank(u, 0, w), B("rW", t)[:, S + LO[c]:S + LO[c] + w], A.is_le), ["UY%d" % c, "rw%d" % t], ["tt%d" % c], [u])
        V(lambda v: v.tensor_tensor(B("sP", t)[:, sl(c)], bank(u, 128, w), B("tt", c)[:], A.is_gt), ["UY%d" % c, "tt%d" % c], ["sp%d%d" % (t, c)], [u])

    def send_phi(t):
        send(t, B("rP", t)[:], B("sP", t)[:], "phi%d" % t, ["sp%d%d" % (t, c) for c in range(NC)], ["rp%d" % t])

    def scatter(t, c):
        lt, n = T["L%d%d" % (t, c)], WID[c] // 16
        V(lambda v: v.tensor_tensor(T.xs[:, :].indirect(lt[:, n:2 * n]), B("na", c)[:], B("nx", c)[:], A.add),
          ["L%d" % c, "na%d" % c, "nx%d" % c], ["xs"])

    def cupd(t, c):
        V(lambda v: v.tensor_tensor(B("ct", c)[:], T.az[:, :].indirect(T["rL%d%d" % (t, c)][:]), B("mk", c)[:], A.mult),
          ["az", "rl%d%d" % (t, c), "mk%d" % c], ["ct%d" % c])
        V(lambda v: v.tensor_tensor(T.cf[:, sl(c)], B("ct", c)[:], B("ck", c)[:], A.add), ["ct%d" % c, "ck%d" % c], ["cf%d" % c])
        if t < RO - 1:
            V(lambda v: v.tensor_copy(T.cu[:, sl(c)], T.cf[:, sl(c)]), ["cf%d" % c], ["cu%d" % c])

    def move1(phi, pk, rb, rk, pb, m):
        V(lambda v: v.tensor_tensor(pb[:], phi[:], rb[:], A.mult), [rk] + pk, [pb.name])
        mm([(bank(m, 0, S), T.bo[:], pb[:], True, True)], ["bo", pb.name], ["rf"], [m])
        mm([(bank(m + 1, 0, S), T.idn[:], rb[:], True, False), (bank(m + 1, 0, S), T.ni[:], pb[:], False, False)],
           ["idn", "ni", rk, pb.name], ["RR"], [m + 1])

    def move2(rb, rk, tb, m):
        V(lambda v: v.tensor_tensor(tb[:], bank(m, 0, S), rb[:], A.is_gt), ["rf", rk], [tb.name], [m])
        mm([(bank(m + 1, 0, S), T.idn[:], tb[:], False, True)], ["idn", tb.name], ["RR"], [m + 1])

    def rup1(t):
        move1(B("rP", t), ["rp%d" % t], T.rb, "rb", T.p1, 0)
        mm([(bank(0, 192, S), T.bo[:], B("rP", t)[:], True, True)], ["bo", "rp%d" % t], ["Fo"], [0])

    def rup2(t):
        move2(T.rb, "rb", T.t1, 0)

    def rup3(t):
        V(lambda v: v.tensor_copy(T.rb2[:], bank(1, 0, S)), ["RR"], ["rb2"], [1])
        move1(B("sP", t), ["sp%d%d" % (t, c) for c in range(NC)], T.rb2, "rb2", T.p1, 2)

    def rup4(t):
        move2(T.rb2, "rb2", T.t1, 2)

    def last_orders1():
        sp = B("sP", RO - 1)
        sk = ["sp%d%d" % (RO - 1, c) for c in range(NC)]
        V(lambda v: v.tensor_tensor(T.p1[:], sp[:], T.rb[:], A.mult), ["rb"] + sk, ["p1"])
        mm([(bank(2, 0, S), T.bo[:], T.p1[:], True, True)], ["bo", "p1"], ["rf"], [2])
        V(lambda v: v.tensor_tensor(T.t1[:], bank(2, 0, S), T.rb[:], A.is_gt), ["rf", "rb"], ["t1"], [2])
        m = [(T.idn[:], T.rb[:]), (T.ni[:], T.p1[:]), (T.idn[:], T.t1[:])]
        seq = []
        for out, terms in ((bank(7, 0, S), m + [(T.mtmp[:, 128:256], sp[:])]), (bank(6, 0, S), m),
                           (bank(6, 192, S), m + [(T.nb[:], sp[:]), (T.idn[:], sp[:])])):
            seq += [(out, l, r, i == 0, i == len(terms) - 1) for i, (l, r) in enumerate(terms)]
        mm(seq, ["idn", "ni", "nb", "mt1", "rb", "p1", "t1"] + sk, ["MK"], [6, 7])
        SC(lambda s: s.activation(T.rb2[:], bank(7, 0, S), F.Copy), ["MK"], ["rb2"], [7])

    def last_orders2():
        rp = B("rP", RO - 1)
        rk = ["rp%d" % (RO - 1)]
        V(lambda v: v.tensor_tensor(T.p1[:], rp[:], bank(6, 0, S), A.mult), ["MK"] + rk, ["p1"], [6])
        mm([(bank(5, 0, S), T.bo[:], T.p1[:], True, True)], ["bo", "p1"], ["m1f"], [5])
        V(lambda v: v.tensor_tensor(T.t1[:], rp[:], bank(6, 192, S), A.mult), ["MK"] + rk, ["t1"], [6])
        V(lambda v: v.tensor_tensor(bank(0, 0, S), bank(6, 0, S), T.t1[:], A.subtract), ["MK", "t1"], ["dd"], [6, 0])
        V(lambda v: v.tensor_tensor(T.p1[:], bank(5, 0, S), T.rb2[:], A.is_gt), ["m1f", "rb2"], ["p1"], [5])
        V(lambda v: v.tensor_tensor(T.rout[:, 0:S], T.p1[:], bank(0, 0, S), A.add), ["p1", "dd"], ["rout"], [0])
        dma("Y", T.ypref[:], T.rout[:, 0:S], "o2", ["rout"], [])
        mm([(bank(4, 192, S), T.bo[:], rp[:], True, True)], ["bo"] + rk, ["Fo"], [4])
        V(lambda v: v.tensor_tensor(T.rout[:, S:2 * S], bank(4, 192, S), T.a32[:], A.add), ["Fo", "a32"], ["aout"], [4])
        dma("S", T.yfail[:], T.rout[0:128:16, S:2 * S], "o3", ["aout"], [])

    def rup5(t):
        SC(lambda s: s.activation(T.rb[:], bank(3, 0, S), F.Copy), ["RR"], ["rb"], [3])

    def aup(t):
        V(lambda v: v.tensor_tensor(T.a32[:], bank(0, 192, S), T.a32[:], A.add), ["Fo"], ["a32"], [0])

    cb = OPT["cb"]
    if OPT["sq"]:
        cb = 0
    for t in range(RO):
        if t == 0:
            gx("S", 0, 0)
            gx("V", 0, 1)
            x0dup(0)
            orders()
            gx("S", 1, 0)
            wdup(t, 0)
            for a in range(4):
                spk_cmp(0, a)
            x0dup(1)
            wdup(t, 1)
            counts()
            thr(t)
        else:
            x0dup(0)
            cupd(t - 1, 1)
            gx("S", 1, 0)
            for a in range(4):
                spk_cmp(0, a)
            wdup(t, 0)
            wcopy(t, 0)
            x0dup(1)
            wdup(t, 1)
            for a in range(cb):
                spk_cmp(1, a)
        for a in range(4):
            spk_wt(0, a)
            spk_y(0, a)
            spk_relu(0, a)
            if a > 0:
                spk_sum(0, a - 1)
        for a in range(4):
            if t == 0 or a >= cb:
                spk_cmp(1, a)
            spk_wt(1, a)
            spk_y(1, a)
            if a < OPT["vr"]:
                spk_relu(1, a)
            if a == 0:
                spk_sum(0, 3)
            elif a <= OPT["vr"]:
                spk_sum(1, a - 1)
            if a == OPT["nda"]:
                spk_nd(t, 0)
        for a in range(OPT["vr"], 4):
            spk_relu(1, a)
            spk_sum(1, a)
        if OPT["vr"] == 4:
            spk_sum(1, 3)
        spk_nd(t, 1)
        if t == 0:
            late_constants()
        else:
            wcopy(t, 1)
            rup1(t - 1)
        for a in range(4):
            mask_f(0, a)
        gy("V", 0, 0)
        gy("S", 0, 1)
        if t > 0:
            rup2(t - 1)
            aup(t - 1)
            thr(t)
            post_h(t - 1, 1)
        for a in range(4):
            mask_f(1, a)
        gy("S", 1, 0)
        hear_in(t, 0)
        for a in range(4):
            hear_cmp(0, a)
            if a == 0:
                hear_nd(t, 0)
            hear_cnt(t, 0, a)
            if a == 1:
                hear_in(t, 1)
        mask_k(0)
        pick1(t, 0)
        hear_b(t, 0)
        hear_b(t, 1)
        pick2(t, 0)
        mask_m(0)
        hear_b(t, 2)
        hear_b(t, 3)
        pick1(t, 1)
        if t > 0:
            rup3(t - 1)
        mask_k(1)
        hear_px(t, 0)
        pick3(t, 0)
        post_y(t, 0)
        hear_nx(t, 0)
        if t < RO - 1:
            post_na(t, 0)
        mask3(0)
        pick2(t, 1)
        if t > 0:
            rup4(t - 1)
        post_h(t, 0)
        hear_px(t, 1)
        hear_pw(t, 0)
        hear_pw(t, 1)
        pick3(t, 1)
        post_y(t, 1)
        if t > 0:
            rup5(t - 1)
        if t < RO - 1:
            post_na(t, 1)
        post_un(t, 0)
        post_un(t, 1)
        post_phi(t, 0)
        post_phi(t, 1)
        send_phi(t)
        hear_nx(t, 1)
        if t < RO - 1:
            scatter(t, 0)
            scatter(t, 1)
        mask_m(1)
        cupd(t, 0)
        mask3(1)
        if t < RO - 1:
            gx("V", 0, 0)
            gx("S", 0, 1)
        else:
            post_h(t, 1)
            dma("Y", T.ycand[:], T.hf[:], "o1", ["hf0", "hf1"], [])
            last_orders1()
    cupd(RO - 1, 1)
    dma("Y", T.yctx[:], T.cf[:], "o0", ["cf0", "cf1"], [])
    last_orders2()
    for s in ("o0", "o1", "o2", "o3"):
        g.sync.wait_ge(T.sem[s], 16)
    for q in ("V", "S", "P", "G"):
        K["need"]("G", (QS[q], K["cnt"][q]))
    g.wait_ge(T.sem["loc"], nloc[0])
